import numpy as np
import ml_dtypes


def mxq(x, axis, fmt="e4m3"):
    dtype, down = {"e4m3": (ml_dtypes.float8_e4m3fn, 7), "e5m2": (ml_dtypes.float8_e5m2, 14)}[fmt]
    v = np.moveaxis(np.asarray(x, np.float32).astype(ml_dtypes.bfloat16).astype(np.float64), axis, -1)
    blocks = v.reshape(v.shape[:-1] + (-1, 32))
    amax = np.abs(blocks).max(-1, keepdims=True)
    byte = np.maximum(np.where(amax > 0, np.frexp(amax)[1] - 1 + 127, 0) - down, 1)
    scale = np.exp2(byte - 127.0)
    codes = (blocks / scale).astype(np.float32).astype(dtype).astype(np.float64)
    return np.moveaxis((codes * scale).reshape(v.shape), -1, axis)


WIDE = False


def mx_kscale(k):
    if not WIDE:
        return np.ones(k)
    levels = np.array([10, -10, 5, -5, 0])
    if k % 512:
        return np.exp2(np.random.permutation(np.resize(levels, k // 32))).repeat(32)
    a = np.empty((k // 512, 16))
    for p in range(k // 512):
        a[p, :8] = np.random.permutation(np.resize(levels, 8))
        for g in range(8):
            far = levels[np.abs(levels - a[p, g]) >= 10]
            a[p, g + 8] = far[np.random.randint(len(far))]
    return np.exp2(a.ravel()).repeat(32)


def f64(x):
    return np.asarray(x).astype(np.float64)


def striped(idx):
    return np.tile(idx.reshape(-1, 16).T, (8, 1)).astype(np.uint16)


def unstriped(offs):
    return offs[:16].T.reshape(-1).astype(np.int64)


def gelu(v):
    return 0.5 * v * (1.0 + np.tanh(np.sqrt(2.0 / np.pi) * (v + 0.044715 * v**3)))


K, T, S, H, N = 512, 4096, 1536, 512, 256


def setup_inputs():
    n = np.random.standard_normal
    s = mx_kscale(K)[:, None]
    u = mx_kscale(H)
    return {
        "xT": (n((K, T)) * s).astype(np.float32),
        "w1": (n((K, H)) / np.sqrt(K) / s).astype(np.float32),
        "w3": (n((K, H)) / np.sqrt(K) / s * u).astype(np.float32),
        "w2": (n((H, N)) / np.sqrt(H) / u[:, None]).astype(np.float32),
        "offs": striped(np.sort(np.random.permutation(T)[:S])),
    }


def reference(xT, w1, w3, w2, offs):
    idx = unstriped(offs)
    xq = mxq(f64(xT)[:, idx], 0, "e4m3")
    h = gelu(mxq(f64(w1), 0, "e4m3").T @ xq) * (mxq(f64(w3), 0, "e4m3").T @ xq)
    y = mxq(f64(w2), 0, "e4m3").T @ mxq(h, 0, "e4m3")
    return y

@@ -1,0 +1,184 @@
+from contextlib import ExitStack
+
+import concourse.mybir as mybir
+
+K, T, S, H, N = 512, 4096, 1536, 512, 256
+FLOPS = 2 * S * (2 * K * H + H * N)
+
+F32 = mybir.dt.float32
+BF16 = mybir.dt.bfloat16
+U32 = mybir.dt.uint32
+I32 = mybir.dt.int32
+U16 = mybir.dt.uint16
+U8 = mybir.dt.uint8
+FP8X4 = mybir.dt.float8_e4m3fn_x4
+GELU = mybir.ActivationFunctionType.Gelu_apprx_tanh
+MULT = mybir.AluOpType.mult
+ADD = mybir.AluOpType.add
+
+P = 128
+PACK = 4
+SUB = 128
+CHUNKS = ((512,"v",),(512,"s",),(512,"v",),(512,"s",),(512,"v",),(256,"s",),(128,"v",),(256,"s",),(256,"s",),(256,"s",),(256,"s",),(128,"v",),)
+SLICES = ((0,384,),(384,896,),(896,1536,),)
+TEXT = ("x0","x1","x2","x3","x4","x5","x6","g0","x7","x8","w1","u0","g1","x9","x10","x11","w3","w2","r0","g2","u1","r1","u2","r2",)
+LOADS = ("x0","offs","x1","x2","x3","x4","x5","x6","x7","x8","w1","x9","x10","x11","w3","w2",)
+W_ENGINES = {"w1": "sg", "w3": "gs", "w2": "g"}
+Y_ENGINES = "s" * 12
+
+
+def tile_picked_pick_glu_gelu_srt_e_kernel(tc, xT, w1, w3, w2, offs, out):
+    nc = tc.nc
+
+    def copy(engine, dst, src):
+        if engine == "v":
+            nc.vector.tensor_copy(dst, src)
+        elif engine == "s":
+            nc.scalar.copy(dst, src)
+        else:
+            nc.gpsimd.tensor_scalar(dst, src, 1.0, 0.0, MULT, ADD)
+
+    with ExitStack() as ctx:
+        keep = ctx.enter_context(tc.tile_pool(name="keep", bufs=1))
+        hidden = ctx.enter_context(tc.tile_pool(name="hidden", bufs=3))
+        gates = ctx.enter_context(tc.tile_pool(name="gates", bufs=12))
+        psum = ctx.enter_context(tc.psum_pool(name="psum", bufs=3))
+        psum_y = ctx.enter_context(tc.psum_pool(name="psum_y", bufs=2))
+
+        offsets = keep.tile([P, S // 16], U16, name="offsets")
+        warm = keep.tile([P, 2], F32, name="warm")
+        codes = keep.tile([P, T], U32, name="codes", align_bytes=64)
+        planes = keep.tile([P, T], U8, name="planes", align_bytes=64)
+        wt = {}
+        for name, src, cols in (("w1", w1, H), ("w3", w3, H), ("w2", w2, N)):
+            raw = keep.tile([P, PACK, cols], F32, name=name + "_raw")
+            bf = keep.tile([P, cols * PACK], BF16, name=name + "_bf", align_bytes=64)
+            wc = keep.tile([P, cols], U32, name=name + "_codes", align_bytes=64)
+            ws = keep.tile([P, cols], U8, name=name + "_planes", align_bytes=64)
+            wt[name] = (raw, bf, wc, ws, src.rearrange("(p j) c -> p j c", j=PACK))
+
+        tokens = xT.rearrange("(p j) t -> p j t", j=PACK)
+        raws = []
+        starts = []
+        at = 0
+        for c, (size, engine) in enumerate(CHUNKS):
+            raw = keep.tile([P, PACK, size], F32, name="raw%d" % c)
+            raws.append(raw)
+            starts.append(at)
+            at += size
+
+        nc.vector.memset(warm[:], 0.0)
+        nc.scalar.activation(warm[:, 1:2], warm[:, 0:1], GELU)
+        nc.gpsimd.memset(planes[:].bitcast(I32), 0)
+
+        for item in LOADS:
+            if item == "offs":
+                nc.sync.dma_start(offsets[:], offs)
+            elif item in wt:
+                nc.sync.dma_start(wt[item][0][:], wt[item][4])
+            else:
+                c = int(item[1:])
+                nc.sync.dma_start(raws[c][:], tokens[:, :, starts[c] : starts[c] + CHUNKS[c][0]])
+
+        picked = {}
+        gelus = {}
+
+        def chunk(c):
+            size, engine = CHUNKS[c]
+            g = keep.tile([P, size, PACK], BF16, name="grouped%d" % c, align_bytes=64)
+            copy(engine, g[:].rearrange("p (c i) j -> p c j i", i=4), raws[c][:].rearrange("p j (c i) -> p c j i", i=4))
+            cols = slice(starts[c], starts[c] + size)
+            nc.vector.quantize_mx(codes[:, cols].bitcast(FP8X4), planes[:, cols], g[:].rearrange("p w j -> p (w j)"))
+
+        def weight(name):
+            raw, bf, wc, ws, _ = wt[name]
+            engines = W_ENGINES[name]
+            if name == "w2":
+                copy(engines[0], bf[:].rearrange("p (c i j) -> p c j i", i=4, j=PACK), raw[:].rearrange("p j (c i) -> p c j i", i=4))
+                nc.vector.quantize_mx(wc[:].bitcast(FP8X4), ws[:], bf[:])
+                return
+            for u in range(2):
+                half = slice(u * 1024, (u + 1) * 1024)
+                copy(engines[u], bf[:, half].rearrange("p (t m j) -> p m t j", t=2, j=PACK),
+                     raw[:].rearrange("p j (m t) -> p m t j", t=PACK)[:, :, 2 * u : 2 * u + 2, :])
+            for u in range(2):
+                half = slice(u * 1024, (u + 1) * 1024)
+                cols = slice(u * 256, (u + 1) * 256)
+                nc.vector.quantize_mx(wc[:, cols].bitcast(FP8X4), ws[:, cols], bf[:, half])
+
+        def gather(s):
+            a, b = SLICES[s]
+            window = T - S + b
+            words = keep.tile([P, b - a], U32, name="words%d" % s, align_bytes=64)
+            scales = keep.tile([P, b - a], U8, name="scales%d" % s, align_bytes=64)
+            picked[s] = (words, scales)
+            places = offsets[:, a // 16 : b // 16]
+            nc.vector.tensor_copy(words[:], codes[:, 0:window].indirect(places))
+            nc.vector.tensor_copy(scales[:], planes[:, 0:window].indirect(places))
+
+        def product(bank, name, s, j):
+            words, scales = picked[s]
+            wc, ws = wt[name][2], wt[name][3]
+            for t in range(PACK):
+                cols = slice(t * P, (t + 1) * P)
+                nc.tensor.matmul_mx(
+                    out=bank[:, cols],
+                    lhsT=wc[:, cols].bitcast(FP8X4), lhsT_scale=ws[:, cols],
+                    rhs=words[:, j : j + SUB].bitcast(FP8X4), rhs_scale=scales[:, j : j + SUB],
+                    start=True, stop=True)
+
+        def up(s):
+            a, b = SLICES[s]
+            for j in range(0, b - a, SUB):
+                g = gates.tile([P, SUB, PACK], F32, name="g")
+                gelus[s, j] = g
+                bank = psum.tile([P, PACK, SUB], F32, name="bank1")
+                product(bank[:].rearrange("p t n -> p (t n)"), "w1", s, j)
+                nc.scalar.activation(g[:], bank[:].rearrange("p t n -> p n t"), GELU)
+
+        def down(s):
+            a, b = SLICES[s]
+            j = 0
+            while j < b - a:
+                n = min(2 * SUB, b - a - j)
+                h = hidden.tile([P, 2 * SUB, PACK], BF16, name="h", align_bytes=64)
+                for q in range(0, n, SUB):
+                    bank = psum.tile([P, PACK, SUB], F32, name="bank3")
+                    product(bank[:].rearrange("p t n -> p (t n)"), "w3", s, j + q)
+                    nc.vector.tensor_tensor(h[:, q : q + SUB, :], bank[:].rearrange("p t n -> p n t"), gelus[s, j + q][:], MULT)
+                h_codes = hidden.tile([P, 2 * SUB], U32, name="h_codes", align_bytes=64)
+                h_planes = hidden.tile([P, 2 * SUB], U8, name="h_planes", align_bytes=64)
+                nc.vector.quantize_mx(h_codes[:, 0:n].bitcast(FP8X4), h_planes[:, 0:n], h[:, 0:n, :].rearrange("p n t -> p (n t)"))
+                y = psum_y.tile([P, 2, 2 * SUB], F32, name="y")
+                wc, ws = wt["w2"][2], wt["w2"][3]
+                for m in range(N // P):
+                    cols = slice(m * P, (m + 1) * P)
+                    nc.tensor.matmul_mx(
+                        out=y[:, m, 0:n],
+                        lhsT=wc[:, cols].bitcast(FP8X4), lhsT_scale=ws[:, cols],
+                        rhs=h_codes[:, 0:n].bitcast(FP8X4), rhs_scale=h_planes[:, 0:n],
+                        start=True, stop=True)
+                j0 = a + j
+                view = out.rearrange("(m p) n -> p m n", p=P)[:, :, j0 : j0 + n]
+                j += n
+                if j0 + n == S:
+                    for m in range(2):
+                        y_half = hidden.tile([P, 2 * SUB], F32, name="y_half%d" % m)
+                        copy("vs"[m], y_half[:, 0:n], y[:, m, 0:n])
+                        nc.sync.dma_start(view[:, m, :], y_half[:, 0:n])
+                else:
+                    y_sb = hidden.tile([P, 2, 2 * SUB], F32, name="y_sb")
+                    copy(Y_ENGINES[j0 // SUB], y_sb[:, :, 0:n], y[:, :, 0:n])
+                    nc.sync.dma_start(view, y_sb[:, :, 0:n])
+
+        for item in TEXT:
+            if item[0] == "x":
+                chunk(int(item[1:]))
+            elif item[0] == "w":
+                weight(item)
+            elif item[0] == "g":
+                gather(int(item[1:]))
+            elif item[0] == "u":
+                up(int(item[1:]))
+            else:
+                down(int(item[1:]))

@@ -19,12 +19,9 @@ ADD = mybir.AluOpType.add
 P = 128
 PACK = 4
 SUB = 128
-CHUNKS = ((512,"v",),(512,"s",),(512,"v",),(512,"s",),(512,"v",),(256,"s",),(128,"v",),(256,"s",),(256,"s",),(256,"s",),(256,"s",),(128,"v",),)
-SLICES = ((0,384,),(384,896,),(896,1536,),)
-TEXT = ("x0","x1","x2","x3","x4","x5","x6","g0","x7","x8","w1","u0","g1","x9","x10","x11","w3","w2","r0","g2","u1","r1","u2","r2",)
-LOADS = ("x0","offs","x1","x2","x3","x4","x5","x6","x7","x8","w1","x9","x10","x11","w3","w2",)
-W_ENGINES = {"w1": "sg", "w3": "gs", "w2": "g"}
-Y_ENGINES = "s" * 12
+CHUNKS = (1024, 512, 512, 512, 256, 128, 256, 256, 256, 256, 128)
+SLICES = ((0, 384), (384, 896), (896, 1536))
+GROUPS = ((0, 2), (2, 4), (4, 6), (6, 8), (8, 10), (10, 12))
 
 
 def tile_picked_pick_glu_gelu_srt_e_kernel(tc, xT, w1, w3, w2, offs, out):
@@ -40,9 +37,7 @@ def tile_picked_pick_glu_gelu_srt_e_kernel(tc, xT, w1, w3, w2, offs, out):
 
     with ExitStack() as ctx:
         keep = ctx.enter_context(tc.tile_pool(name="keep", bufs=1))
-        hidden = ctx.enter_context(tc.tile_pool(name="hidden", bufs=3))
-        gates = ctx.enter_context(tc.tile_pool(name="gates", bufs=12))
-        psum = ctx.enter_context(tc.psum_pool(name="psum", bufs=3))
+        psum1 = ctx.enter_context(tc.psum_pool(name="psum1", bufs=6))
         psum_y = ctx.enter_context(tc.psum_pool(name="psum_y", bufs=2))
 
         offsets = keep.tile([P, S // 16], U16, name="offsets")
@@ -51,134 +46,259 @@ def tile_picked_pick_glu_gelu_srt_e_kernel(tc, xT, w1, w3, w2, offs, out):
         planes = keep.tile([P, T], U8, name="planes", align_bytes=64)
         wt = {}
         for name, src, cols in (("w1", w1, H), ("w3", w3, H), ("w2", w2, N)):
-            raw = keep.tile([P, PACK, cols], F32, name=name + "_raw")
-            bf = keep.tile([P, cols * PACK], BF16, name=name + "_bf", align_bytes=64)
+            raw = keep.tile([P, PACK, cols], F32, name=name + "_raw", tag=name + "_raw", align_bytes=64)
+            bf = keep.tile([P, cols * PACK], BF16, name=name + "_bf", tag=name + "_bf", align_bytes=64)
             wc = keep.tile([P, cols], U32, name=name + "_codes", align_bytes=64)
             ws = keep.tile([P, cols], U8, name=name + "_planes", align_bytes=64)
             wt[name] = (raw, bf, wc, ws, src.rearrange("(p j) c -> p j c", j=PACK))
 
         tokens = xT.rearrange("(p j) t -> p j t", j=PACK)
         raws = []
+        groupeds = []
         starts = []
         at = 0
-        for c, (size, engine) in enumerate(CHUNKS):
-            raw = keep.tile([P, PACK, size], F32, name="raw%d" % c)
-            raws.append(raw)
+        for c, size in enumerate(CHUNKS):
+            raws.append(keep.tile([P, PACK, size], F32, name="raw%d" % c, tag="raw%d" % c, align_bytes=64))
+            groupeds.append(keep.tile([P, size, PACK], BF16, name="grouped%d" % c, align_bytes=64))
             starts.append(at)
             at += size
 
         nc.vector.memset(warm[:], 0.0)
         nc.scalar.activation(warm[:, 1:2], warm[:, 0:1], GELU)
-        nc.gpsimd.memset(planes[:].bitcast(I32), 0)
+        nc.vector.memset(planes[:].bitcast(I32), 0)
 
-        for item in LOADS:
-            if item == "offs":
-                nc.sync.dma_start(offsets[:], offs)
-            elif item in wt:
-                nc.sync.dma_start(wt[item][0][:], wt[item][4])
-            else:
-                c = int(item[1:])
-                nc.sync.dma_start(raws[c][:], tokens[:, :, starts[c] : starts[c] + CHUNKS[c][0]])
+        def load_x(c):
+            nc.sync.dma_start(raws[c][:], tokens[:, :, starts[c] : starts[c] + CHUNKS[c]])
+
+        def load_w(name):
+            nc.sync.dma_start(wt[name][0][:], wt[name][4])
+
+        load_x(0)
+        nc.sync.dma_start(offsets[:], offs)
+        load_x(1)
+        load_x(2)
+        load_x(3)
+        load_x(4)
+        load_x(5)
+        load_x(6)
+        load_x(7)
+        load_w("w1")
+        load_w("w3")
+        load_x(8)
+        load_x(9)
+        load_x(10)
+        load_w("w2")
 
         picked = {}
         gelus = {}
+        hiddens = {}
+        h_quant = {}
 
-        def chunk(c):
-            size, engine = CHUNKS[c]
-            g = keep.tile([P, size, PACK], BF16, name="grouped%d" % c, align_bytes=64)
-            copy(engine, g[:].rearrange("p (c i) j -> p c j i", i=4), raws[c][:].rearrange("p j (c i) -> p c j i", i=4))
-            cols = slice(starts[c], starts[c] + size)
-            nc.vector.quantize_mx(codes[:, cols].bitcast(FP8X4), planes[:, cols], g[:].rearrange("p w j -> p (w j)"))
+        def round_x(c, engine, lo=0, hi=None):
+            hi = CHUNKS[c] if hi is None else hi
+            copy(engine, groupeds[c][:, lo:hi, :].rearrange("p (c i) j -> p c j i", i=4),
+                 raws[c][:, :, lo:hi].rearrange("p j (c i) -> p c j i", i=4))
 
-        def weight(name):
-            raw, bf, wc, ws, _ = wt[name]
-            engines = W_ENGINES[name]
-            if name == "w2":
-                copy(engines[0], bf[:].rearrange("p (c i j) -> p c j i", i=4, j=PACK), raw[:].rearrange("p j (c i) -> p c j i", i=4))
-                nc.vector.quantize_mx(wc[:].bitcast(FP8X4), ws[:], bf[:])
-                return
-            for u in range(2):
-                half = slice(u * 1024, (u + 1) * 1024)
-                copy(engines[u], bf[:, half].rearrange("p (t m j) -> p m t j", t=2, j=PACK),
-                     raw[:].rearrange("p j (m t) -> p m t j", t=PACK)[:, :, 2 * u : 2 * u + 2, :])
-            for u in range(2):
-                half = slice(u * 1024, (u + 1) * 1024)
-                cols = slice(u * 256, (u + 1) * 256)
-                nc.vector.quantize_mx(wc[:, cols].bitcast(FP8X4), ws[:, cols], bf[:, half])
+        def quant_x(c, lo=0, hi=None):
+            hi = CHUNKS[c] if hi is None else hi
+            cols = slice(starts[c] + lo, starts[c] + hi)
+            nc.vector.quantize_mx(codes[:, cols].bitcast(FP8X4), planes[:, cols], groupeds[c][:, lo:hi, :].rearrange("p w j -> p (w j)"))
+
+        def round_w(name, engine, lo=0, hi=P):
+            raw, bf = wt[name][0], wt[name][1]
+            copy(engine, bf[:].rearrange("p (t m j) -> p m j t", t=PACK, j=PACK)[:, lo:hi],
+                 raw[:].rearrange("p j (m t) -> p m j t", t=PACK)[:, lo:hi])
+
+        def round_w2(engine):
+            raw, bf = wt["w2"][0], wt["w2"][1]
+            if engine == "g":
+                copy(engine, bf[:].rearrange("p (c j) -> p c j", j=PACK), raw[:].rearrange("p j c -> p c j"))
+            else:
+                copy(engine, bf[:].rearrange("p (c i j) -> p c j i", i=4, j=PACK), raw[:].rearrange("p j (c i) -> p c j i", i=4))
+
+        def quant_w(name):
+            nc.vector.quantize_mx(wt[name][2][:].bitcast(FP8X4), wt[name][3][:], wt[name][1][:])
+
+        slices = {}
+
+        def gather_words(s, tag=None):
+            a, b = SLICES[s]
+            slices[s] = keep.tile([P, b - a], U32, name="words%d" % s, tag=tag or "words%d" % s, align_bytes=64)
+            nc.vector.tensor_copy(slices[s][:], codes[:, 0 : T - S + b].indirect(offsets[:, a // 16 : b // 16]))
+
+        def gather_scales(s, tag):
+            a, b = SLICES[s]
+            scales = keep.tile([P, b - a], U8, name="scales%d" % s, tag=tag, align_bytes=64)
+            nc.vector.tensor_copy(scales[:], planes[:, 0 : T - S + b].indirect(offsets[:, a // 16 : b // 16]))
+            for j in range(a, b, SUB):
+                picked[j // SUB] = (slices[s][:, j - a : j - a + SUB], scales[:, j - a : j - a + SUB])
 
         def gather(s):
-            a, b = SLICES[s]
-            window = T - S + b
-            words = keep.tile([P, b - a], U32, name="words%d" % s, align_bytes=64)
-            scales = keep.tile([P, b - a], U8, name="scales%d" % s, align_bytes=64)
-            picked[s] = (words, scales)
-            places = offsets[:, a // 16 : b // 16]
-            nc.vector.tensor_copy(words[:], codes[:, 0:window].indirect(places))
-            nc.vector.tensor_copy(scales[:], planes[:, 0:window].indirect(places))
+            gather_words(s)
+            gather_scales(s, "scales%d" % s)
 
-        def product(bank, name, s, j):
-            words, scales = picked[s]
+        def product(bank, name, i):
+            words, scales = picked[i]
             wc, ws = wt[name][2], wt[name][3]
             for t in range(PACK):
                 cols = slice(t * P, (t + 1) * P)
                 nc.tensor.matmul_mx(
-                    out=bank[:, cols],
+                    out=bank[:, t, :],
                     lhsT=wc[:, cols].bitcast(FP8X4), lhsT_scale=ws[:, cols],
-                    rhs=words[:, j : j + SUB].bitcast(FP8X4), rhs_scale=scales[:, j : j + SUB],
+                    rhs=words.bitcast(FP8X4), rhs_scale=scales,
                     start=True, stop=True)
 
-        def up(s):
-            a, b = SLICES[s]
-            for j in range(0, b - a, SUB):
-                g = gates.tile([P, SUB, PACK], F32, name="g")
-                gelus[s, j] = g
-                bank = psum.tile([P, PACK, SUB], F32, name="bank1")
-                product(bank[:].rearrange("p t n -> p (t n)"), "w1", s, j)
-                nc.scalar.activation(g[:], bank[:].rearrange("p t n -> p n t"), GELU)
+        def gates(lo, hi, tag):
+            g = keep.tile([P, (hi - lo) * SUB, PACK], F32, name="g%d" % lo, tag=tag, align_bytes=64)
+            for i in range(lo, hi):
+                gelus[i] = g[:, (i - lo) * SUB : (i - lo + 1) * SUB, :]
 
-        def down(s):
-            a, b = SLICES[s]
-            j = 0
-            while j < b - a:
-                n = min(2 * SUB, b - a - j)
-                h = hidden.tile([P, 2 * SUB, PACK], BF16, name="h", align_bytes=64)
-                for q in range(0, n, SUB):
-                    bank = psum.tile([P, PACK, SUB], F32, name="bank3")
-                    product(bank[:].rearrange("p t n -> p (t n)"), "w3", s, j + q)
-                    nc.vector.tensor_tensor(h[:, q : q + SUB, :], bank[:].rearrange("p t n -> p n t"), gelus[s, j + q][:], MULT)
-                h_codes = hidden.tile([P, 2 * SUB], U32, name="h_codes", align_bytes=64)
-                h_planes = hidden.tile([P, 2 * SUB], U8, name="h_planes", align_bytes=64)
-                nc.vector.quantize_mx(h_codes[:, 0:n].bitcast(FP8X4), h_planes[:, 0:n], h[:, 0:n, :].rearrange("p n t -> p (n t)"))
-                y = psum_y.tile([P, 2, 2 * SUB], F32, name="y")
-                wc, ws = wt["w2"][2], wt["w2"][3]
-                for m in range(N // P):
+        def up(i):
+            g = gelus[i]
+            bank = psum1.tile([P, PACK, SUB], F32, name="bank1", tag="bank1")
+            product(bank, "w1", i)
+            nc.scalar.activation(g, bank[:].rearrange("p t n -> p n t"), GELU)
+
+        group_of = {}
+        for q, (lo, hi) in enumerate(GROUPS):
+            hiddens[q] = keep.tile([P, (hi - lo) * SUB, PACK], BF16, name="h%d" % q, align_bytes=64)
+            for i in range(lo, hi):
+                group_of[i] = q
+
+        linear = {}
+
+        def lin(i):
+            linear[i] = psum1.tile([P, PACK, SUB], F32, name="bank3", tag="bank1")
+            product(linear[i], "w3", i)
+
+        def mult(i):
+            q = group_of[i]
+            at = (i - GROUPS[q][0]) * SUB
+            nc.vector.tensor_tensor(hiddens[q][:, at : at + SUB, :], linear[i][:].rearrange("p t n -> p n t"), gelus[i], MULT)
+
+        def quant_h(q):
+            n = (GROUPS[q][1] - GROUPS[q][0]) * SUB
+            h_codes = keep.tile([P, n], U32, name="h_codes%d" % q, align_bytes=64)
+            h_planes = keep.tile([P, n], U8, name="h_planes%d" % q, align_bytes=64)
+            h_quant[q] = (h_codes, h_planes)
+            nc.vector.quantize_mx(h_codes[:].bitcast(FP8X4), h_planes[:], hiddens[q][:].rearrange("p n t -> p (n t)"))
+
+        def down(q, engines, late=False):
+            n = (GROUPS[q][1] - GROUPS[q][0]) * SUB
+            h_codes, h_planes = h_quant[q]
+            wc, ws = wt["w2"][2], wt["w2"][3]
+            j0 = GROUPS[q][0] * SUB
+            view = out.rearrange("(m p) n -> p m n", p=P)[:, :, j0 : j0 + n]
+            if len(engines) == 2:
+                for m in range(2):
+                    y = psum1.tile([P, 2, 2 * SUB], F32, name="y", tag="bank1") if late else psum_y.tile([P, 2, 2 * SUB], F32, name="y")
                     cols = slice(m * P, (m + 1) * P)
                     nc.tensor.matmul_mx(
-                        out=y[:, m, 0:n],
+                        out=y[:].rearrange("p m n -> p (m n)")[:, 0:n],
                         lhsT=wc[:, cols].bitcast(FP8X4), lhsT_scale=ws[:, cols],
-                        rhs=h_codes[:, 0:n].bitcast(FP8X4), rhs_scale=h_planes[:, 0:n],
+                        rhs=h_codes[:].bitcast(FP8X4), rhs_scale=h_planes[:],
                         start=True, stop=True)
-                j0 = a + j
-                view = out.rearrange("(m p) n -> p m n", p=P)[:, :, j0 : j0 + n]
-                j += n
-                if j0 + n == S:
-                    for m in range(2):
-                        y_half = hidden.tile([P, 2 * SUB], F32, name="y_half%d" % m)
-                        copy("vs"[m], y_half[:, 0:n], y[:, m, 0:n])
-                        nc.sync.dma_start(view[:, m, :], y_half[:, 0:n])
-                else:
-                    y_sb = hidden.tile([P, 2, 2 * SUB], F32, name="y_sb")
-                    copy(Y_ENGINES[j0 // SUB], y_sb[:, :, 0:n], y[:, :, 0:n])
-                    nc.sync.dma_start(view, y_sb[:, :, 0:n])
+                    y_half = keep.tile([P, n], F32, name="y_half%d_%d" % (q, m))
+                    copy(engines[m], y_half[:], y[:].rearrange("p m n -> p (m n)")[:, 0:n])
+                    nc.sync.dma_start(view[:, m, :], y_half[:])
+                return
+            y = psum_y.tile([P, 2, 2 * SUB], F32, name="y")
+            for m in range(N // P):
+                cols = slice(m * P, (m + 1) * P)
+                nc.tensor.matmul_mx(
+                    out=y[:, m, 0:n],
+                    lhsT=wc[:, cols].bitcast(FP8X4), lhsT_scale=ws[:, cols],
+                    rhs=h_codes[:].bitcast(FP8X4), rhs_scale=h_planes[:],
+                    start=True, stop=True)
+            y_sb = keep.tile([P, 2, n], F32, name="y_sb%d" % q)
+            copy(engines, y_sb[:], y[:, :, 0:n])
+            nc.sync.dma_start(view, y_sb[:])
 
-        for item in TEXT:
-            if item[0] == "x":
-                chunk(int(item[1:]))
-            elif item[0] == "w":
-                weight(item)
-            elif item[0] == "g":
-                gather(int(item[1:]))
-            elif item[0] == "u":
-                up(int(item[1:]))
-            else:
-                down(int(item[1:]))
+        round_x(0,"v",0,512)
+        round_x(0,"s",512,1024)
+        quant_x(0,0,512)
+        quant_x(0,512,1024)
+        round_x(1,"v")
+        quant_x(1)
+        round_x(2,"v")
+        quant_x(2)
+        round_x(3,"v",0,256)
+        round_x(3,"s",256,512)
+        quant_x(3,0,256)
+        round_x(4,"v")
+        quant_x(3,256,512)
+        round_x(5,"s")
+        quant_x(4)
+        quant_x(5)
+        gather(0)
+        round_x(6,"s")
+        round_x(7,"s")
+        quant_x(6)
+        quant_x(7)
+        gather(1)
+        round_w("w1","s",0,128)
+        quant_w("w1")
+        round_w("w3","s",0,64)
+        round_w("w3","v",64,128)
+        quant_w("w3")
+        gates(0,3,"w3_raw")
+        up(0)
+        up(1)
+        round_x(8,"s")
+        up(2)
+        lin(0)
+        lin(1)
+        lin(2)
+        mult(0)
+        round_x(9,"v")
+        mult(1)
+        quant_x(8)
+        round_x(10,"s")
+        mult(2)
+        quant_x(9)
+        quant_x(10)
+        round_w2("s")
+        gates(3,7,"raw10")
+        up(3)
+        up(4)
+        up(5)
+        up(6)
+        lin(3)
+        lin(4)
+        lin(5)
+        lin(6)
+        quant_h(0)
+        gather_words(2)
+        quant_w("w2")
+        down(0,"s")
+        gather_scales(2,"scales2")
+        gates(7,12,"g7")
+        up(7)
+        up(8)
+        mult(3)
+        lin(7)
+        mult(4)
+        up(9)
+        quant_h(1)
+        down(1,"s")
+        mult(5)
+        lin(8)
+        mult(6)
+        up(10)
+        lin(9)
+        quant_h(2)
+        down(2,"s")
+        up(11)
+        mult(7)
+        lin(10)
+        mult(8)
+        lin(11)
+        quant_h(3)
+        down(3,"s")
+        mult(9)
+        mult(10)
+        quant_h(4)
+        down(4,"s")
+        mult(11)
+        quant_h(5)
+        down(5,"vs",True)

@@ -19,7 +19,7 @@ ADD = mybir.AluOpType.add
 P = 128
 PACK = 4
 SUB = 128
-CHUNKS = (1024, 512, 512, 512, 256, 128, 256, 256, 256, 256, 128)
+CHUNKS = (1024, 1024, 512, 384, 512, 256, 256, 128)
 SLICES = ((0, 384), (384, 896), (896, 1536))
 GROUPS = ((0, 2), (2, 4), (4, 6), (6, 8), (8, 10), (10, 12))
 
@@ -79,14 +79,11 @@ def tile_picked_pick_glu_gelu_srt_e_kernel(tc, xT, w1, w3, w2, offs, out):
         load_x(2)
         load_x(3)
         load_x(4)
+        load_w("w1")
+        load_w("w3")
         load_x(5)
         load_x(6)
         load_x(7)
-        load_w("w1")
-        load_w("w3")
-        load_x(8)
-        load_x(9)
-        load_x(10)
         load_w("w2")
 
         picked = {}
@@ -218,25 +215,24 @@ def tile_picked_pick_glu_gelu_srt_e_kernel(tc, xT, w1, w3, w2, offs, out):
         round_x(0,"s",512,1024)
         quant_x(0,0,512)
         quant_x(0,512,1024)
-        round_x(1,"v")
-        quant_x(1)
-        round_x(2,"v")
-        quant_x(2)
-        round_x(3,"v",0,256)
-        round_x(3,"s",256,512)
+        round_x(1,"v",0,512)
+        round_x(1,"s",512,1024)
+        quant_x(1,0,512)
+        quant_x(1,512,1024)
+        round_x(2,"v",0,256)
+        round_x(2,"s",256,512)
+        quant_x(2,0,512)
+        round_x(3,"v",0,192)
+        round_x(3,"s",192,384)
         quant_x(3,0,256)
-        round_x(4,"v")
-        quant_x(3,256,512)
-        round_x(5,"s")
-        quant_x(4)
-        quant_x(5)
+        quant_x(3,256,384)
         gather(0)
-        round_x(6,"s")
-        round_x(7,"s")
-        quant_x(6)
-        quant_x(7)
+        round_x(4,"s",256,512)
+        round_x(4,"v",0,256)
+        quant_x(4)
         gather(1)
-        round_w("w1","s",0,128)
+        round_w("w1","s",0,96)
+        round_w("w1","v",96,128)
         quant_w("w1")
         round_w("w3","s",0,64)
         round_w("w3","v",64,128)
@@ -244,21 +240,21 @@ def tile_picked_pick_glu_gelu_srt_e_kernel(tc, xT, w1, w3, w2, offs, out):
         gates(0,3,"w3_raw")
         up(0)
         up(1)
-        round_x(8,"s")
+        round_x(5,"s")
         up(2)
         lin(0)
         lin(1)
         lin(2)
         mult(0)
-        round_x(9,"v")
+        round_x(6,"v")
         mult(1)
-        quant_x(8)
-        round_x(10,"s")
+        quant_x(5)
+        round_x(7,"s")
         mult(2)
-        quant_x(9)
-        quant_x(10)
+        quant_x(6)
+        quant_x(7)
         round_w2("s")
-        gates(3,7,"raw10")
+        gates(3,7,"raw7")
         up(3)
         up(4)
         up(5)

@@ -93,8 +93,8 @@ def tile_picked_pick_glu_gelu_srt_e_kernel(tc, xT, w1, w3, w2, offs, out):
 
         def round_x(c, engine, lo=0, hi=None):
             hi = CHUNKS[c] if hi is None else hi
-            copy(engine, groupeds[c][:, lo:hi, :].rearrange("p (c i) j -> p c j i", i=4),
-                 raws[c][:, :, lo:hi].rearrange("p j (c i) -> p c j i", i=4))
+            copy(engine, groupeds[c][:, lo:hi, :].rearrange("p (c i) j -> p c j i", i=2),
+                 raws[c][:, :, lo:hi].rearrange("p j (c i) -> p c j i", i=2))
 
         def quant_x(c, lo=0, hi=None):
             hi = CHUNKS[c] if hi is None else hi
@@ -111,7 +111,7 @@ def tile_picked_pick_glu_gelu_srt_e_kernel(tc, xT, w1, w3, w2, offs, out):
             if engine == "g":
                 copy(engine, bf[:].rearrange("p (c j) -> p c j", j=PACK), raw[:].rearrange("p j c -> p c j"))
             else:
-                copy(engine, bf[:].rearrange("p (c i j) -> p c j i", i=4, j=PACK), raw[:].rearrange("p j (c i) -> p c j i", i=4))
+                copy(engine, bf[:].rearrange("p (c i j) -> p c j i", i=2, j=PACK), raw[:].rearrange("p j (c i) -> p c j i", i=2))
 
         def quant_w(name):
             nc.vector.quantize_mx(wt[name][2][:].bitcast(FP8X4), wt[name][3][:], wt[name][1][:])

@@ -18,10 +18,10 @@ ADD = mybir.AluOpType.add
 
 P = 128
 PACK = 4
-SUB = 128
-CHUNKS = (1024, 1024, 512, 384, 512, 256, 256, 128)
+BLOCK = 128
+LOADS = (1024, 1024, 512, 384, 512, 256, 256, 128)
 SLICES = ((0, 384), (384, 896), (896, 1536))
-GROUPS = ((0, 2), (2, 4), (4, 6), (6, 8), (8, 10), (10, 12))
+GROUPS = ((0, 2), (2, 4), (4, 6), (6, 8), (8, 9), (9, 10), (10, 11), (11, 12))
 
 
 def tile_picked_pick_glu_gelu_srt_e_kernel(tc, xT, w1, w3, w2, offs, out):
@@ -37,7 +37,7 @@ def tile_picked_pick_glu_gelu_srt_e_kernel(tc, xT, w1, w3, w2, offs, out):
 
     with ExitStack() as ctx:
         keep = ctx.enter_context(tc.tile_pool(name="keep", bufs=1))
-        psum1 = ctx.enter_context(tc.psum_pool(name="psum1", bufs=6))
+        ring = ctx.enter_context(tc.psum_pool(name="ring", bufs=6))
         psum_y = ctx.enter_context(tc.psum_pool(name="psum_y", bufs=2))
 
         offsets = keep.tile([P, S // 16], U16, name="offsets")
@@ -54,12 +54,12 @@ def tile_picked_pick_glu_gelu_srt_e_kernel(tc, xT, w1, w3, w2, offs, out):
 
         tokens = xT.rearrange("(p j) t -> p j t", j=PACK)
         raws = []
-        groupeds = []
+        rounded = []
         starts = []
         at = 0
-        for c, size in enumerate(CHUNKS):
+        for c, size in enumerate(LOADS):
             raws.append(keep.tile([P, PACK, size], F32, name="raw%d" % c, tag="raw%d" % c, align_bytes=64))
-            groupeds.append(keep.tile([P, size, PACK], BF16, name="grouped%d" % c, align_bytes=64))
+            rounded.append(keep.tile([P, size, PACK], BF16, name="rounded%d" % c, tag="rounded%d" % c, align_bytes=64))
             starts.append(at)
             at += size
 
@@ -68,7 +68,7 @@ def tile_picked_pick_glu_gelu_srt_e_kernel(tc, xT, w1, w3, w2, offs, out):
         nc.vector.memset(planes[:].bitcast(I32), 0)
 
         def load_x(c):
-            nc.sync.dma_start(raws[c][:], tokens[:, :, starts[c] : starts[c] + CHUNKS[c]])
+            nc.sync.dma_start(raws[c][:], tokens[:, :, starts[c] : starts[c] + LOADS[c]])
 
         def load_w(name):
             nc.sync.dma_start(wt[name][0][:], wt[name][4])
@@ -88,51 +88,55 @@ def tile_picked_pick_glu_gelu_srt_e_kernel(tc, xT, w1, w3, w2, offs, out):
 
         picked = {}
         gelus = {}
+        linear = {}
         hiddens = {}
         h_quant = {}
+        slices = {}
+        slice_scales = {}
 
         def round_x(c, engine, lo=0, hi=None):
-            hi = CHUNKS[c] if hi is None else hi
-            copy(engine, groupeds[c][:, lo:hi, :].rearrange("p (c i) j -> p c j i", i=2),
+            hi = LOADS[c] if hi is None else hi
+            copy(engine, rounded[c][:, lo:hi, :].rearrange("p (c i) j -> p c j i", i=2),
                  raws[c][:, :, lo:hi].rearrange("p j (c i) -> p c j i", i=2))
 
         def quant_x(c, lo=0, hi=None):
-            hi = CHUNKS[c] if hi is None else hi
+            hi = LOADS[c] if hi is None else hi
             cols = slice(starts[c] + lo, starts[c] + hi)
-            nc.vector.quantize_mx(codes[:, cols].bitcast(FP8X4), planes[:, cols], groupeds[c][:, lo:hi, :].rearrange("p w j -> p (w j)"))
+            nc.vector.quantize_mx(codes[:, cols].bitcast(FP8X4), planes[:, cols], rounded[c][:, lo:hi, :].rearrange("p w j -> p (w j)"))
 
-        def round_w(name, engine, lo=0, hi=P):
+        def round_w(name, engine, lo=0, hi=P, t0=0, t1=PACK):
             raw, bf = wt[name][0], wt[name][1]
-            copy(engine, bf[:].rearrange("p (t m j) -> p m j t", t=PACK, j=PACK)[:, lo:hi],
-                 raw[:].rearrange("p j (m t) -> p m j t", t=PACK)[:, lo:hi])
+            copy(engine, bf[:].rearrange("p (t m j) -> p m j t", t=PACK, j=PACK)[:, lo:hi, :, t0:t1],
+                 raw[:].rearrange("p j (m t) -> p m j t", t=PACK)[:, lo:hi, :, t0:t1])
 
-        def round_w2(engine):
+        def round_w2(engine, lo=0, hi=N):
             raw, bf = wt["w2"][0], wt["w2"][1]
             if engine == "g":
-                copy(engine, bf[:].rearrange("p (c j) -> p c j", j=PACK), raw[:].rearrange("p j c -> p c j"))
+                copy(engine, bf[:].rearrange("p (c j) -> p c j", j=PACK)[:, lo:hi], raw[:].rearrange("p j c -> p c j")[:, lo:hi])
             else:
-                copy(engine, bf[:].rearrange("p (c i j) -> p c j i", i=2, j=PACK), raw[:].rearrange("p j (c i) -> p c j i", i=2))
+                copy(engine, bf[:].rearrange("p (c i j) -> p c j i", i=2, j=PACK)[:, lo // 2 : hi // 2],
+                     raw[:].rearrange("p j (c i) -> p c j i", i=2)[:, lo // 2 : hi // 2])
 
-        def quant_w(name):
-            nc.vector.quantize_mx(wt[name][2][:].bitcast(FP8X4), wt[name][3][:], wt[name][1][:])
-
-        slices = {}
+        def quant_w(name, lo=0, hi=None):
+            hi = wt[name][2].shape[1] if hi is None else hi
+            nc.vector.quantize_mx(wt[name][2][:, lo:hi].bitcast(FP8X4), wt[name][3][:, lo:hi], wt[name][1][:, PACK * lo : PACK * hi])
 
         def gather_words(s, tag=None):
             a, b = SLICES[s]
             slices[s] = keep.tile([P, b - a], U32, name="words%d" % s, tag=tag or "words%d" % s, align_bytes=64)
             nc.vector.tensor_copy(slices[s][:], codes[:, 0 : T - S + b].indirect(offsets[:, a // 16 : b // 16]))
 
-        def gather_scales(s, tag):
+        def gather_scales(s, tag=None):
             a, b = SLICES[s]
-            scales = keep.tile([P, b - a], U8, name="scales%d" % s, tag=tag, align_bytes=64)
+            scales = keep.tile([P, b - a], U8, name="scales%d" % s, tag=tag or "scales%d" % s, align_bytes=64)
             nc.vector.tensor_copy(scales[:], planes[:, 0 : T - S + b].indirect(offsets[:, a // 16 : b // 16]))
-            for j in range(a, b, SUB):
-                picked[j // SUB] = (slices[s][:, j - a : j - a + SUB], scales[:, j - a : j - a + SUB])
+            slice_scales[s] = scales
+            for j in range(a, b, BLOCK):
+                picked[j // BLOCK] = (slices[s][:, j - a : j - a + BLOCK], scales[:, j - a : j - a + BLOCK])
 
         def gather(s):
             gather_words(s)
-            gather_scales(s, "scales%d" % s)
+            gather_scales(s)
 
         def product(bank, name, i):
             words, scales = picked[i]
@@ -145,116 +149,135 @@ def tile_picked_pick_glu_gelu_srt_e_kernel(tc, xT, w1, w3, w2, offs, out):
                     rhs=words.bitcast(FP8X4), rhs_scale=scales,
                     start=True, stop=True)
 
-        def gates(lo, hi, tag):
-            g = keep.tile([P, (hi - lo) * SUB, PACK], F32, name="g%d" % lo, tag=tag, align_bytes=64)
+        def warm_up(s, passes):
+            bank = psum_y.tile([P, 2, 2 * BLOCK], F32, name="y", tag="y")
+            words, scales = slices[s], slice_scales[s]
+            for k in range(passes):
+                nc.tensor.matmul_mx(
+                    out=bank[:, k % 2, :],
+                    lhsT=words[:, 0:P].bitcast(FP8X4), lhsT_scale=scales[:, 0:P],
+                    rhs=words[:, 0 : 2 * BLOCK].bitcast(FP8X4), rhs_scale=scales[:, 0 : 2 * BLOCK],
+                    start=True, stop=True)
+
+        def gates(lo, hi, tag=None):
+            g = keep.tile([P, (hi - lo) * BLOCK, PACK], F32, name="g%d" % lo, tag=tag or "g%d" % lo, align_bytes=64)
             for i in range(lo, hi):
-                gelus[i] = g[:, (i - lo) * SUB : (i - lo + 1) * SUB, :]
+                gelus[i] = g[:, (i - lo) * BLOCK : (i - lo + 1) * BLOCK, :]
 
         def up(i):
-            g = gelus[i]
-            bank = psum1.tile([P, PACK, SUB], F32, name="bank1", tag="bank1")
+            bank = ring.tile([P, PACK, BLOCK], F32, name="bank1", tag="ring")
             product(bank, "w1", i)
-            nc.scalar.activation(g, bank[:].rearrange("p t n -> p n t"), GELU)
+            nc.scalar.activation(gelus[i], bank[:].rearrange("p t n -> p n t"), GELU)
+
+        def lin(i):
+            linear[i] = ring.tile([P, PACK, BLOCK], F32, name="bank3", tag="ring")
+            product(linear[i], "w3", i)
 
         group_of = {}
         for q, (lo, hi) in enumerate(GROUPS):
-            hiddens[q] = keep.tile([P, (hi - lo) * SUB, PACK], BF16, name="h%d" % q, align_bytes=64)
             for i in range(lo, hi):
                 group_of[i] = q
 
-        linear = {}
-
-        def lin(i):
-            linear[i] = psum1.tile([P, PACK, SUB], F32, name="bank3", tag="bank1")
-            product(linear[i], "w3", i)
+        def hidden(q, tag=None):
+            lo, hi = GROUPS[q]
+            hiddens[q] = keep.tile([P, (hi - lo) * BLOCK, PACK], BF16, name="h%d" % q, tag=tag or "h%d" % q, align_bytes=64)
 
         def mult(i):
             q = group_of[i]
-            at = (i - GROUPS[q][0]) * SUB
-            nc.vector.tensor_tensor(hiddens[q][:, at : at + SUB, :], linear[i][:].rearrange("p t n -> p n t"), gelus[i], MULT)
+            if q not in hiddens:
+                hidden(q)
+            at = (i - GROUPS[q][0]) * BLOCK
+            nc.vector.tensor_tensor(hiddens[q][:, at : at + BLOCK, :], linear[i][:].rearrange("p t n -> p n t"), gelus[i], MULT)
 
-        def quant_h(q):
-            n = (GROUPS[q][1] - GROUPS[q][0]) * SUB
-            h_codes = keep.tile([P, n], U32, name="h_codes%d" % q, align_bytes=64)
+        def mult_g(i):
+            q = group_of[i]
+            if q not in hiddens:
+                hidden(q)
+            at = (i - GROUPS[q][0]) * BLOCK
+            b = keep.tile([P, BLOCK, PACK], F32, name="b%d" % i, align_bytes=64)
+            nc.scalar.copy(b[:], linear[i][:].rearrange("p t n -> p n t"))
+            nc.gpsimd.tensor_tensor(hiddens[q][:, at : at + BLOCK, :], b[:], gelus[i], MULT)
+
+        def quant_h(q, tag=None):
+            n = (GROUPS[q][1] - GROUPS[q][0]) * BLOCK
+            h_codes = keep.tile([P, n], U32, name="h_codes%d" % q, tag=tag or "h_codes%d" % q, align_bytes=64)
             h_planes = keep.tile([P, n], U8, name="h_planes%d" % q, align_bytes=64)
             h_quant[q] = (h_codes, h_planes)
             nc.vector.quantize_mx(h_codes[:].bitcast(FP8X4), h_planes[:], hiddens[q][:].rearrange("p n t -> p (n t)"))
 
-        def down(q, engines, late=False):
-            n = (GROUPS[q][1] - GROUPS[q][0]) * SUB
+        def down(q, engine, pool=psum_y, tag="y"):
+            n = (GROUPS[q][1] - GROUPS[q][0]) * BLOCK
             h_codes, h_planes = h_quant[q]
             wc, ws = wt["w2"][2], wt["w2"][3]
-            j0 = GROUPS[q][0] * SUB
+            j0 = GROUPS[q][0] * BLOCK
             view = out.rearrange("(m p) n -> p m n", p=P)[:, :, j0 : j0 + n]
-            if len(engines) == 2:
-                for m in range(2):
-                    y = psum1.tile([P, 2, 2 * SUB], F32, name="y", tag="bank1") if late else psum_y.tile([P, 2, 2 * SUB], F32, name="y")
-                    cols = slice(m * P, (m + 1) * P)
-                    nc.tensor.matmul_mx(
-                        out=y[:].rearrange("p m n -> p (m n)")[:, 0:n],
-                        lhsT=wc[:, cols].bitcast(FP8X4), lhsT_scale=ws[:, cols],
-                        rhs=h_codes[:].bitcast(FP8X4), rhs_scale=h_planes[:],
-                        start=True, stop=True)
-                    y_half = keep.tile([P, n], F32, name="y_half%d_%d" % (q, m))
-                    copy(engines[m], y_half[:], y[:].rearrange("p m n -> p (m n)")[:, 0:n])
-                    nc.sync.dma_start(view[:, m, :], y_half[:])
-                return
-            y = psum_y.tile([P, 2, 2 * SUB], F32, name="y")
+            y = pool.tile([P, 2, n], F32, name="y", tag=tag)
             for m in range(N // P):
                 cols = slice(m * P, (m + 1) * P)
                 nc.tensor.matmul_mx(
-                    out=y[:, m, 0:n],
+                    out=y[:, m, :],
                     lhsT=wc[:, cols].bitcast(FP8X4), lhsT_scale=ws[:, cols],
                     rhs=h_codes[:].bitcast(FP8X4), rhs_scale=h_planes[:],
                     start=True, stop=True)
             y_sb = keep.tile([P, 2, n], F32, name="y_sb%d" % q)
-            copy(engines, y_sb[:], y[:, :, 0:n])
+            copy(engine, y_sb[:], y[:])
             nc.sync.dma_start(view, y_sb[:])
 
-        round_x(0,"v",0,512)
-        round_x(0,"s",512,1024)
-        quant_x(0,0,512)
-        quant_x(0,512,1024)
-        round_x(1,"v",0,512)
-        round_x(1,"s",512,1024)
-        quant_x(1,0,512)
-        quant_x(1,512,1024)
-        round_x(2,"v",0,256)
-        round_x(2,"s",256,512)
-        quant_x(2,0,512)
-        round_x(3,"v",0,192)
-        round_x(3,"s",192,384)
-        quant_x(3,0,256)
-        quant_x(3,256,384)
+        def probe(tile_ap):
+            clock = keep.tile([P, 1], F32, name="clock", tag="clock")
+            nc.gpsimd.tensor_copy(clock[:], tile_ap)
+
+        round_x(0, "v", 0, 512)
+        round_x(0, "s", 512, 1024)
+        quant_x(0, 0, 512)
+        quant_x(0, 512, 1024)
+        round_x(1, "s", 0, 256)
+        round_x(1, "v", 512, 1024)
+        round_x(1, "s", 256, 512)
+        quant_x(1, 0, 256)
+        quant_x(1, 512, 1024)
+        quant_x(1, 256, 512)
+        round_x(2, "v", 0, 256)
+        round_x(2, "s", 256, 512)
+        quant_x(2, 0, 512)
+        round_x(3, "s", 0, 128)
+        round_x(3, "v", 128, 384)
+        quant_x(3, 0, 128)
+        quant_x(3, 128, 384)
         gather(0)
-        round_x(4,"s",256,512)
-        round_x(4,"v",0,256)
-        quant_x(4)
+        round_x(4, "s", 0, 256)
+        round_x(4, "v", 256, 512)
+        quant_x(4, 0, 256)
+        quant_x(4, 256, 512)
         gather(1)
-        round_w("w1","s",0,96)
-        round_w("w1","v",96,128)
-        quant_w("w1")
-        round_w("w3","s",0,64)
-        round_w("w3","v",64,128)
-        quant_w("w3")
-        gates(0,3,"w3_raw")
+        warm_up(1, 4)
+        round_w("w1", "s", 0, 128, 0, 2)
+        round_w("w1", "s", 0, 64, 2, 4)
+        round_w("w1", "v", 64, 128, 2, 4)
+        quant_w("w1", 0, 256)
+        quant_w("w1", 256, 512)
+        round_w("w3", "s", 0, 128, 0, 2)
+        round_w("w3", "v", 0, 128, 2, 4)
+        quant_w("w3", 0, 256)
+        quant_w("w3", 256, 512)
+        gates(0, 3, "w3_raw")
         up(0)
         up(1)
-        round_x(5,"s")
+        round_x(5, "s")
         up(2)
         lin(0)
         lin(1)
         lin(2)
+        round_x(6, "v")
         mult(0)
-        round_x(6,"v")
         mult(1)
         quant_x(5)
-        round_x(7,"s")
+        round_x(7, "s")
         mult(2)
         quant_x(6)
         quant_x(7)
         round_w2("s")
-        gates(3,7,"raw7")
+        gates(3, 7, "raw7")
         up(3)
         up(4)
         up(5)
@@ -266,9 +289,9 @@ def tile_picked_pick_glu_gelu_srt_e_kernel(tc, xT, w1, w3, w2, offs, out):
         quant_h(0)
         gather_words(2)
         quant_w("w2")
-        down(0,"s")
-        gather_scales(2,"scales2")
-        gates(7,12,"g7")
+        down(0, "s")
+        gather_scales(2)
+        gates(7, 12)
         up(7)
         up(8)
         mult(3)
@@ -276,25 +299,29 @@ def tile_picked_pick_glu_gelu_srt_e_kernel(tc, xT, w1, w3, w2, offs, out):
         mult(4)
         up(9)
         quant_h(1)
-        down(1,"s")
+        down(1, "s")
         mult(5)
         lin(8)
         mult(6)
         up(10)
         lin(9)
         quant_h(2)
-        down(2,"s")
+        down(2, "s")
         up(11)
         mult(7)
         lin(10)
         mult(8)
         lin(11)
         quant_h(3)
-        down(3,"s")
+        down(3, "s")
         mult(9)
-        mult(10)
         quant_h(4)
-        down(4,"s")
-        mult(11)
+        down(4, "s")
+        mult(10)
         quant_h(5)
-        down(5,"vs",True)
+        down(5, "s")
+        mult(11)
+        quant_h(6)
+        quant_h(7)
+        down(6, "s")
+        down(7, "v", ring, "ring")

@@ -8,320 +8,205 @@ FLOPS = 2 * S * (2 * K * H + H * N)
 F32 = mybir.dt.float32
 BF16 = mybir.dt.bfloat16
 U32 = mybir.dt.uint32
-I32 = mybir.dt.int32
 U16 = mybir.dt.uint16
 U8 = mybir.dt.uint8
 FP8X4 = mybir.dt.float8_e4m3fn_x4
 GELU = mybir.ActivationFunctionType.Gelu_apprx_tanh
+COPY = mybir.ActivationFunctionType.Copy
 MULT = mybir.AluOpType.mult
 ADD = mybir.AluOpType.add
 
 P = 128
 PACK = 4
 BLOCK = 128
-LOADS = (1024, 1024, 512, 384, 512, 256, 256, 128)
-SLICES = ((0, 384), (384, 896), (896, 1536))
-GROUPS = ((0, 2), (2, 4), (4, 6), (6, 8), (8, 9), (9, 10), (10, 11), (11, 12))
+BLOCKS = S // BLOCK
+SLICES = ((0, 128), (128, 384), (384, 640), (640, 896), (896, 1152), (1152, 1536))
+PIECES = (128, 384, 896, 1536)
+HELD = 4
+GROUPS = ((0, 2), (2, 4), (4, 6), (6, 8), (8, 10), (10, 11), (11, 12))
+SCALAR_SHARE = {"w1": 192, "w3": 88}
+GELU_LEAD = 3
+LIN_LEAD = 2
 
 
 def tile_picked_pick_glu_gelu_srt_e_kernel(tc, xT, w1, w3, w2, offs, out):
     nc = tc.nc
 
-    def copy(engine, dst, src):
-        if engine == "v":
-            nc.vector.tensor_copy(dst, src)
-        elif engine == "s":
-            nc.scalar.copy(dst, src)
-        else:
-            nc.gpsimd.tensor_scalar(dst, src, 1.0, 0.0, MULT, ADD)
-
     with ExitStack() as ctx:
         keep = ctx.enter_context(tc.tile_pool(name="keep", bufs=1))
-        ring = ctx.enter_context(tc.psum_pool(name="ring", bufs=6))
-        psum_y = ctx.enter_context(tc.psum_pool(name="psum_y", bufs=2))
+        gate_banks = ctx.enter_context(tc.psum_pool(name="gate_banks", bufs=3))
+        lin_banks = ctx.enter_context(tc.psum_pool(name="lin_banks", bufs=3))
+        y_banks = ctx.enter_context(tc.psum_pool(name="y_banks", bufs=2))
 
         offsets = keep.tile([P, S // 16], U16, name="offsets")
         warm = keep.tile([P, 2], F32, name="warm")
-        codes = keep.tile([P, T], U32, name="codes", align_bytes=64)
-        planes = keep.tile([P, T], U8, name="planes", align_bytes=64)
-        wt = {}
+        rows = [keep.tile([P, T], F32, name="row%d" % j, align_bytes=64) for j in range(PACK)]
+        weights = {}
         for name, src, cols in (("w1", w1, H), ("w3", w3, H), ("w2", w2, N)):
             raw = keep.tile([P, PACK, cols], F32, name=name + "_raw", tag=name + "_raw", align_bytes=64)
-            bf = keep.tile([P, cols * PACK], BF16, name=name + "_bf", tag=name + "_bf", align_bytes=64)
-            wc = keep.tile([P, cols], U32, name=name + "_codes", align_bytes=64)
-            ws = keep.tile([P, cols], U8, name=name + "_planes", align_bytes=64)
-            wt[name] = (raw, bf, wc, ws, src.rearrange("(p j) c -> p j c", j=PACK))
-
-        tokens = xT.rearrange("(p j) t -> p j t", j=PACK)
-        raws = []
-        rounded = []
-        starts = []
-        at = 0
-        for c, size in enumerate(LOADS):
-            raws.append(keep.tile([P, PACK, size], F32, name="raw%d" % c, tag="raw%d" % c, align_bytes=64))
-            rounded.append(keep.tile([P, size, PACK], BF16, name="rounded%d" % c, tag="rounded%d" % c, align_bytes=64))
-            starts.append(at)
-            at += size
+            rounded = keep.tile([P, cols * PACK], BF16, name=name + "_rounded", tag="w1_rounded" if name == "w1" else "w3_rounded", align_bytes=64)
+            codes = keep.tile([P, cols], U32, name=name + "_codes", align_bytes=64)
+            scales = keep.tile([P, cols], U8, name=name + "_scales", align_bytes=64)
+            weights[name] = (raw, rounded, codes, scales, src.rearrange("(p j) c -> p j c", j=PACK))
+        early = keep.tile([P, 2, S], BF16, name="early", align_bytes=64)
+        late, quads, x_codes, x_scales = [], [], [], []
+        for s, (a, b) in enumerate(SLICES):
+            late.append(keep.tile([P, 2, b - a], F32, name="late%d" % s, align_bytes=64))
+            quads.append(keep.tile([P, b - a, PACK], BF16, name="quads%d" % s, align_bytes=64))
+            if s < HELD:
+                x_codes.append(keep.tile([P, b - a], U32, name="x_codes%d" % s, align_bytes=64)[:])
+            x_scales.append(keep.tile([P, b - a], U8, name="x_scales%d" % s, align_bytes=64))
 
         nc.vector.memset(warm[:], 0.0)
         nc.scalar.activation(warm[:, 1:2], warm[:, 0:1], GELU)
-        nc.vector.memset(planes[:].bitcast(I32), 0)
 
-        def load_x(c):
-            nc.sync.dma_start(raws[c][:], tokens[:, :, starts[c] : starts[c] + LOADS[c]])
-
-        def load_w(name):
-            nc.sync.dma_start(wt[name][0][:], wt[name][4])
-
-        load_x(0)
+        tokens = xT.rearrange("(p j) t -> p j t", j=PACK)
+        nc.sync.dma_start(rows[0][:], tokens[:, 0, :])
         nc.sync.dma_start(offsets[:], offs)
-        load_x(1)
-        load_x(2)
-        load_x(3)
-        load_x(4)
-        load_w("w1")
-        load_w("w3")
-        load_x(5)
-        load_x(6)
-        load_x(7)
-        load_w("w2")
+        nc.sync.dma_start(rows[1][:], tokens[:, 1, :])
+        nc.sync.dma_start(rows[2][:], tokens[:, 2, :])
+        done = 0
+        for b in PIECES:
+            upto = T - S + b
+            nc.sync.dma_start(rows[3][:, done:upto], tokens[:, 3, done:upto])
+            done = upto
+        for name in ("w1", "w3", "w2"):
+            nc.sync.dma_start(weights[name][0][:], weights[name][4])
 
-        picked = {}
-        gelus = {}
-        linear = {}
-        hiddens = {}
-        h_quant = {}
-        slices = {}
-        slice_scales = {}
-
-        def round_x(c, engine, lo=0, hi=None):
-            hi = LOADS[c] if hi is None else hi
-            copy(engine, rounded[c][:, lo:hi, :].rearrange("p (c i) j -> p c j i", i=2),
-                 raws[c][:, :, lo:hi].rearrange("p j (c i) -> p c j i", i=2))
-
-        def quant_x(c, lo=0, hi=None):
-            hi = LOADS[c] if hi is None else hi
-            cols = slice(starts[c] + lo, starts[c] + hi)
-            nc.vector.quantize_mx(codes[:, cols].bitcast(FP8X4), planes[:, cols], rounded[c][:, lo:hi, :].rearrange("p w j -> p (w j)"))
-
-        def round_w(name, engine, lo=0, hi=P, t0=0, t1=PACK):
-            raw, bf = wt[name][0], wt[name][1]
-            copy(engine, bf[:].rearrange("p (t m j) -> p m j t", t=PACK, j=PACK)[:, lo:hi, :, t0:t1],
-                 raw[:].rearrange("p j (m t) -> p m j t", t=PACK)[:, lo:hi, :, t0:t1])
-
-        def round_w2(engine, lo=0, hi=N):
-            raw, bf = wt["w2"][0], wt["w2"][1]
-            if engine == "g":
-                copy(engine, bf[:].rearrange("p (c j) -> p c j", j=PACK)[:, lo:hi], raw[:].rearrange("p j c -> p c j")[:, lo:hi])
-            else:
-                copy(engine, bf[:].rearrange("p (c i j) -> p c j i", i=2, j=PACK)[:, lo // 2 : hi // 2],
-                     raw[:].rearrange("p j (c i) -> p c j i", i=2)[:, lo // 2 : hi // 2])
-
-        def quant_w(name, lo=0, hi=None):
-            hi = wt[name][2].shape[1] if hi is None else hi
-            nc.vector.quantize_mx(wt[name][2][:, lo:hi].bitcast(FP8X4), wt[name][3][:, lo:hi], wt[name][1][:, PACK * lo : PACK * hi])
-
-        def gather_words(s, tag=None):
+        def entries(s):
             a, b = SLICES[s]
-            slices[s] = keep.tile([P, b - a], U32, name="words%d" % s, tag=tag or "words%d" % s, align_bytes=64)
-            nc.vector.tensor_copy(slices[s][:], codes[:, 0 : T - S + b].indirect(offsets[:, a // 16 : b // 16]))
+            return offsets[:, a // 16 : b // 16]
 
-        def gather_scales(s, tag=None):
+        def place_early(s):
             a, b = SLICES[s]
-            scales = keep.tile([P, b - a], U8, name="scales%d" % s, tag=tag or "scales%d" % s, align_bytes=64)
-            nc.vector.tensor_copy(scales[:], planes[:, 0 : T - S + b].indirect(offsets[:, a // 16 : b // 16]))
-            slice_scales[s] = scales
-            for j in range(a, b, BLOCK):
-                picked[j // BLOCK] = (slices[s][:, j - a : j - a + BLOCK], scales[:, j - a : j - a + BLOCK])
+            nc.vector.tensor_copy(quads[s][:, :, 0:2], early[:, :, a:b].rearrange("p j n -> p n j"))
 
-        def gather(s):
-            gather_words(s)
-            gather_scales(s)
+        def gather_last(s):
+            nc.scalar.activation(late[s][:, 1, :], rows[3][:, 0 : T - S + min(b for b in PIECES if b >= SLICES[s][1])].indirect(entries(s)), COPY)
+
+        def place_late(s):
+            nc.vector.tensor_copy(quads[s][:, :, 2:4], late[s][:].rearrange("p j n -> p n j"))
+
+        def quantise_x(s):
+            nc.vector.quantize_mx(x_codes[s].bitcast(FP8X4), x_scales[s][:], quads[s][:].rearrange("p n j -> p (n j)"))
+
+        def dealt(name, lo, hi, t0):
+            raw, rounded = weights[name][0], weights[name][1]
+            return (rounded[:].rearrange("p (t m j) -> p m j t", t=PACK, j=PACK)[:, lo:hi, :, t0 : t0 + 2],
+                    raw[:].rearrange("p j (m t) -> p m j t", t=PACK)[:, lo:hi, :, t0 : t0 + 2])
+
+        def quantise_w(name, lo, hi):
+            rounded, codes, scales = weights[name][1:4]
+            nc.vector.quantize_mx(codes[:, lo:hi].bitcast(FP8X4), scales[:, lo:hi], rounded[:, PACK * lo : PACK * hi])
+
+        def prepare_w(name):
+            share = SCALAR_SHARE[name]
+            if share > P:
+                nc.scalar.copy(*dealt(name, 0, share - P, 2))
+            nc.scalar.copy(*dealt(name, 0, min(share, P), 0))
+            nc.vector.tensor_copy(*dealt(name, max(share - P, 0), P, 2))
+            if share < P:
+                nc.vector.tensor_copy(*dealt(name, share, P, 0))
+            quantise_w(name, H // 2, H)
+            quantise_w(name, 0, H // 2)
+
+        def round_w2():
+            raw, rounded = weights["w2"][0], weights["w2"][1]
+            nc.gpsimd.tensor_scalar(rounded[:].rearrange("p (c j) -> p c j", j=PACK), raw[:].rearrange("p j c -> p c j"), 1.0, 0.0, MULT, ADD)
 
         def product(bank, name, i):
-            words, scales = picked[i]
-            wc, ws = wt[name][2], wt[name][3]
-            for t in range(PACK):
+            s = max(k for k, (a, b) in enumerate(SLICES) if a <= i * BLOCK)
+            at = i * BLOCK - SLICES[s][0]
+            codes, scales = weights[name][2], weights[name][3]
+            for t in (2, 3, 0, 1):
                 cols = slice(t * P, (t + 1) * P)
                 nc.tensor.matmul_mx(
                     out=bank[:, t, :],
-                    lhsT=wc[:, cols].bitcast(FP8X4), lhsT_scale=ws[:, cols],
-                    rhs=words.bitcast(FP8X4), rhs_scale=scales,
+                    lhsT=codes[:, cols].bitcast(FP8X4), lhsT_scale=scales[:, cols],
+                    rhs=x_codes[s][:, at : at + BLOCK].bitcast(FP8X4), rhs_scale=x_scales[s][:, at : at + BLOCK],
                     start=True, stop=True)
 
-        def warm_up(s, passes):
-            bank = psum_y.tile([P, 2, 2 * BLOCK], F32, name="y", tag="y")
-            words, scales = slices[s], slice_scales[s]
-            for k in range(passes):
-                nc.tensor.matmul_mx(
-                    out=bank[:, k % 2, :],
-                    lhsT=words[:, 0:P].bitcast(FP8X4), lhsT_scale=scales[:, 0:P],
-                    rhs=words[:, 0 : 2 * BLOCK].bitcast(FP8X4), rhs_scale=scales[:, 0 : 2 * BLOCK],
-                    start=True, stop=True)
+        gelus, linears, hiddens = {}, {}, {}
 
-        def gates(lo, hi, tag=None):
-            g = keep.tile([P, (hi - lo) * BLOCK, PACK], F32, name="g%d" % lo, tag=tag or "g%d" % lo, align_bytes=64)
-            for i in range(lo, hi):
-                gelus[i] = g[:, (i - lo) * BLOCK : (i - lo + 1) * BLOCK, :]
-
-        def up(i):
-            bank = ring.tile([P, PACK, BLOCK], F32, name="bank1", tag="ring")
+        def gate(i):
+            bank = gate_banks.tile([P, PACK, BLOCK], F32, name="gate_bank")
             product(bank, "w1", i)
+            if i not in gelus:
+                gelus[i] = keep.tile([P, BLOCK, PACK], F32, name="gelu%d" % i, align_bytes=64)[:]
             nc.scalar.activation(gelus[i], bank[:].rearrange("p t n -> p n t"), GELU)
 
-        def lin(i):
-            linear[i] = ring.tile([P, PACK, BLOCK], F32, name="bank3", tag="ring")
-            product(linear[i], "w3", i)
+        def linear(i):
+            linears[i] = lin_banks.tile([P, PACK, BLOCK], F32, name="lin_bank")
+            product(linears[i], "w3", i)
 
-        group_of = {}
-        for q, (lo, hi) in enumerate(GROUPS):
-            for i in range(lo, hi):
-                group_of[i] = q
-
-        def hidden(q, tag=None):
+        def multiply(q, i):
             lo, hi = GROUPS[q]
-            hiddens[q] = keep.tile([P, (hi - lo) * BLOCK, PACK], BF16, name="h%d" % q, tag=tag or "h%d" % q, align_bytes=64)
+            if i == lo:
+                hiddens[q] = keep.tile([P, (hi - lo) * BLOCK, PACK], BF16, name="hidden%d" % q, align_bytes=64)
+            at = (i - lo) * BLOCK
+            nc.vector.tensor_tensor(hiddens[q][:, at : at + BLOCK, :], linears[i][:].rearrange("p t n -> p n t"), gelus[i], MULT)
 
-        def mult(i):
-            q = group_of[i]
-            if q not in hiddens:
-                hidden(q)
-            at = (i - GROUPS[q][0]) * BLOCK
-            nc.vector.tensor_tensor(hiddens[q][:, at : at + BLOCK, :], linear[i][:].rearrange("p t n -> p n t"), gelus[i], MULT)
-
-        def mult_g(i):
-            q = group_of[i]
-            if q not in hiddens:
-                hidden(q)
-            at = (i - GROUPS[q][0]) * BLOCK
-            b = keep.tile([P, BLOCK, PACK], F32, name="b%d" % i, align_bytes=64)
-            nc.scalar.copy(b[:], linear[i][:].rearrange("p t n -> p n t"))
-            nc.gpsimd.tensor_tensor(hiddens[q][:, at : at + BLOCK, :], b[:], gelus[i], MULT)
-
-        def quant_h(q, tag=None):
-            n = (GROUPS[q][1] - GROUPS[q][0]) * BLOCK
-            h_codes = keep.tile([P, n], U32, name="h_codes%d" % q, tag=tag or "h_codes%d" % q, align_bytes=64)
-            h_planes = keep.tile([P, n], U8, name="h_planes%d" % q, align_bytes=64)
-            h_quant[q] = (h_codes, h_planes)
-            nc.vector.quantize_mx(h_codes[:].bitcast(FP8X4), h_planes[:], hiddens[q][:].rearrange("p n t -> p (n t)"))
-
-        def down(q, engine, pool=psum_y, tag="y"):
-            n = (GROUPS[q][1] - GROUPS[q][0]) * BLOCK
-            h_codes, h_planes = h_quant[q]
-            wc, ws = wt["w2"][2], wt["w2"][3]
-            j0 = GROUPS[q][0] * BLOCK
-            view = out.rearrange("(m p) n -> p m n", p=P)[:, :, j0 : j0 + n]
-            y = pool.tile([P, 2, n], F32, name="y", tag=tag)
+        def finish(q):
+            lo, hi = GROUPS[q]
+            n = (hi - lo) * BLOCK
+            h_codes = keep.tile([P, n], U32, name="h_codes%d" % q, align_bytes=64)
+            h_scales = keep.tile([P, n], U8, name="h_scales%d" % q, align_bytes=64)
+            nc.vector.quantize_mx(h_codes[:].bitcast(FP8X4), h_scales[:], hiddens[q][:].rearrange("p n t -> p (n t)"))
+            codes, scales = weights["w2"][2], weights["w2"][3]
+            y = y_banks.tile([P, N // P, n], F32, name="y_bank")
             for m in range(N // P):
                 cols = slice(m * P, (m + 1) * P)
                 nc.tensor.matmul_mx(
                     out=y[:, m, :],
-                    lhsT=wc[:, cols].bitcast(FP8X4), lhsT_scale=ws[:, cols],
-                    rhs=h_codes[:].bitcast(FP8X4), rhs_scale=h_planes[:],
+                    lhsT=codes[:, cols].bitcast(FP8X4), lhsT_scale=scales[:, cols],
+                    rhs=h_codes[:].bitcast(FP8X4), rhs_scale=h_scales[:],
                     start=True, stop=True)
-            y_sb = keep.tile([P, 2, n], F32, name="y_sb%d" % q)
-            copy(engine, y_sb[:], y[:])
-            nc.sync.dma_start(view, y_sb[:])
+            y_out = keep.tile([P, N // P, n], F32, name="y_out%d" % q)
+            if q == len(GROUPS) - 1:
+                nc.vector.tensor_copy(y_out[:], y[:])
+            else:
+                nc.scalar.copy(y_out[:], y[:])
+            nc.sync.dma_start(out.rearrange("(m p) n -> p m n", p=P)[:, :, lo * BLOCK : hi * BLOCK], y_out[:])
 
-        def probe(tile_ap):
-            clock = keep.tile([P, 1], F32, name="clock", tag="clock")
-            nc.gpsimd.tensor_copy(clock[:], tile_ap)
+        for j in (0, 1):
+            nc.scalar.activation(early[:, j, :], rows[j][:].indirect(offsets[:]), COPY)
+        for s in range(len(SLICES)):
+            place_early(s)
+        for s in range(HELD):
+            nc.scalar.activation(late[s][:, 0, :], rows[2][:].indirect(entries(s)), COPY)
+        for s in range(HELD, len(SLICES)):
+            nc.vector.tensor_copy(late[s][:, 0, :], rows[2][:].indirect(entries(s)))
+        for s in range(len(SLICES)):
+            gather_last(s)
+            place_late(s)
+            if 0 < s <= HELD:
+                quantise_x(s - 1)
+        prepare_w("w1")
 
-        round_x(0, "v", 0, 512)
-        round_x(0, "s", 512, 1024)
-        quant_x(0, 0, 512)
-        quant_x(0, 512, 1024)
-        round_x(1, "s", 0, 256)
-        round_x(1, "v", 512, 1024)
-        round_x(1, "s", 256, 512)
-        quant_x(1, 0, 256)
-        quant_x(1, 512, 1024)
-        quant_x(1, 256, 512)
-        round_x(2, "v", 0, 256)
-        round_x(2, "s", 256, 512)
-        quant_x(2, 0, 512)
-        round_x(3, "s", 0, 128)
-        round_x(3, "v", 128, 384)
-        quant_x(3, 0, 128)
-        quant_x(3, 128, 384)
-        gather(0)
-        round_x(4, "s", 0, 256)
-        round_x(4, "v", 256, 512)
-        quant_x(4, 0, 256)
-        quant_x(4, 256, 512)
-        gather(1)
-        warm_up(1, 4)
-        round_w("w1", "s", 0, 128, 0, 2)
-        round_w("w1", "s", 0, 64, 2, 4)
-        round_w("w1", "v", 64, 128, 2, 4)
-        quant_w("w1", 0, 256)
-        quant_w("w1", 256, 512)
-        round_w("w3", "s", 0, 128, 0, 2)
-        round_w("w3", "v", 0, 128, 2, 4)
-        quant_w("w3", 0, 256)
-        quant_w("w3", 256, 512)
-        gates(0, 3, "w3_raw")
-        up(0)
-        up(1)
-        round_x(5, "s")
-        up(2)
-        lin(0)
-        lin(1)
-        lin(2)
-        round_x(6, "v")
-        mult(0)
-        mult(1)
-        quant_x(5)
-        round_x(7, "s")
-        mult(2)
-        quant_x(6)
-        quant_x(7)
-        round_w2("s")
-        gates(3, 7, "raw7")
-        up(3)
-        up(4)
-        up(5)
-        up(6)
-        lin(3)
-        lin(4)
-        lin(5)
-        lin(6)
-        quant_h(0)
-        gather_words(2)
-        quant_w("w2")
-        down(0, "s")
-        gather_scales(2)
-        gates(7, 12)
-        up(7)
-        up(8)
-        mult(3)
-        lin(7)
-        mult(4)
-        up(9)
-        quant_h(1)
-        down(1, "s")
-        mult(5)
-        lin(8)
-        mult(6)
-        up(10)
-        lin(9)
-        quant_h(2)
-        down(2, "s")
-        up(11)
-        mult(7)
-        lin(10)
-        mult(8)
-        lin(11)
-        quant_h(3)
-        down(3, "s")
-        mult(9)
-        quant_h(4)
-        down(4, "s")
-        mult(10)
-        quant_h(5)
-        down(5, "s")
-        mult(11)
-        quant_h(6)
-        quant_h(7)
-        down(6, "s")
-        down(7, "v", ring, "ring")
+        held = keep.tile([P, S - SLICES[HELD][0]], U32, name="held", tag="w1_raw", align_bytes=64)
+        for s in range(HELD, len(SLICES)):
+            x_codes.append(held[:, SLICES[s][0] - SLICES[HELD][0] : SLICES[s][1] - SLICES[HELD][0]])
+            quantise_x(s)
+        prepare_w("w3")
+        round_w2()
+        first = keep.tile([P, GELU_LEAD * BLOCK, PACK], F32, name="first", tag="w3_raw", align_bytes=64)
+        for i in range(GELU_LEAD):
+            gelus[i] = first[:, i * BLOCK : (i + 1) * BLOCK, :]
+            gate(i)
+        for i in range(LIN_LEAD):
+            linear(i)
+        pending = None
+        for q, (lo, hi) in enumerate(GROUPS):
+            for i in range(lo, hi):
+                if i + GELU_LEAD < BLOCKS:
+                    gate(i + GELU_LEAD)
+                if i + LIN_LEAD < BLOCKS:
+                    linear(i + LIN_LEAD)
+                multiply(q, i)
+                if i == 1:
+                    quantise_w("w2", 0, N)
+                if pending is not None:
+                    finish(pending)
+                    pending = None
+            pending = q
+        finish(pending)

@@ -14,7 +14,6 @@ FP8X4 = mybir.dt.float8_e4m3fn_x4
 GELU = mybir.ActivationFunctionType.Gelu_apprx_tanh
 COPY = mybir.ActivationFunctionType.Copy
 MULT = mybir.AluOpType.mult
-ADD = mybir.AluOpType.add
 
 P = 128
 PACK = 4
@@ -44,10 +43,10 @@ def tile_picked_pick_glu_gelu_srt_e_kernel(tc, xT, w1, w3, w2, offs, out):
         weights = {}
         for name, src, cols in (("w1", w1, H), ("w3", w3, H), ("w2", w2, N)):
             raw = keep.tile([P, PACK, cols], F32, name=name + "_raw", tag=name + "_raw", align_bytes=64)
-            rounded = keep.tile([P, cols * PACK], BF16, name=name + "_rounded", tag="w1_rounded" if name == "w1" else "w3_rounded", align_bytes=64)
-            codes = keep.tile([P, cols], U32, name=name + "_codes", align_bytes=64)
+            rounded = keep.tile([P, cols * PACK], BF16, name=name + "_rounded", align_bytes=64)
+            codes = keep.tile([P, cols], U32, name=name + "_codes", align_bytes=64) if name != "w2" else None
             scales = keep.tile([P, cols], U8, name=name + "_scales", align_bytes=64)
-            weights[name] = (raw, rounded, codes, scales, src.rearrange("(p j) c -> p j c", j=PACK))
+            weights[name] = [raw, rounded, codes, scales, src.rearrange("(p j) c -> p j c", j=PACK)]
         early = keep.tile([P, 2, S], BF16, name="early", align_bytes=64)
         late, quads, x_codes, x_scales = [], [], [], []
         for s, (a, b) in enumerate(SLICES):
@@ -112,7 +111,8 @@ def tile_picked_pick_glu_gelu_srt_e_kernel(tc, xT, w1, w3, w2, offs, out):
 
         def round_w2():
             raw, rounded = weights["w2"][0], weights["w2"][1]
-            nc.gpsimd.tensor_scalar(rounded[:].rearrange("p (c j) -> p c j", j=PACK), raw[:].rearrange("p j c -> p c j"), 1.0, 0.0, MULT, ADD)
+            nc.vector.tensor_copy(rounded[:].rearrange("p (c i j) -> p c j i", i=2, j=PACK),
+                                  raw[:].rearrange("p j (c i) -> p c j i", i=2))
 
         def product(bank, name, i):
             s = max(k for k, (a, b) in enumerate(SLICES) if a <= i * BLOCK)
@@ -203,7 +203,9 @@ def tile_picked_pick_glu_gelu_srt_e_kernel(tc, xT, w1, w3, w2, offs, out):
                 if i + LIN_LEAD < BLOCKS:
                     linear(i + LIN_LEAD)
                 multiply(q, i)
-                if i == 1:
+                if i == GELU_LEAD - 1:
+                    w2_codes = keep.tile([P, N], U32, name="w2_codes", tag="w3_raw", align_bytes=64)
+                    weights["w2"][2] = w2_codes
                     quantise_w("w2", 0, N)
                 if pending is not None:
                     finish(pending)

@@ -23,7 +23,8 @@ SLICES = ((0, 128), (128, 384), (384, 640), (640, 896), (896, 1152), (1152, 1536
 PIECES = (128, 384, 896, 1536)
 HELD = 4
 GROUPS = ((0, 2), (2, 4), (4, 6), (6, 8), (8, 10), (10, 11), (11, 12))
-SCALAR_SHARE = {"w1": 192, "w3": 88}
+W1_SCALAR = 96
+W3_SCALAR = 44
 GELU_LEAD = 3
 LIN_LEAD = 2
 
@@ -40,17 +41,18 @@ def tile_picked_pick_glu_gelu_srt_e_kernel(tc, xT, w1, w3, w2, offs, out):
         offsets = keep.tile([P, S // 16], U16, name="offsets")
         warm = keep.tile([P, 2], F32, name="warm")
         rows = [keep.tile([P, T], F32, name="row%d" % j, align_bytes=64) for j in range(PACK)]
-        weights = {}
-        for name, src, cols in (("w1", w1, H), ("w3", w3, H), ("w2", w2, N)):
-            raw = keep.tile([P, PACK, cols], F32, name=name + "_raw", tag=name + "_raw", align_bytes=64)
-            rounded = keep.tile([P, cols * PACK], BF16, name=name + "_rounded", align_bytes=64)
-            codes = keep.tile([P, cols], U32, name=name + "_codes", align_bytes=64) if name != "w2" else None
-            scales = keep.tile([P, cols], U8, name=name + "_scales", align_bytes=64)
-            weights[name] = [raw, rounded, codes, scales, src.rearrange("(p j) c -> p j c", j=PACK)]
-        early = keep.tile([P, 2, S], BF16, name="early", align_bytes=64)
-        late, quads, x_codes, x_scales = [], [], [], []
+        raws, roundeds, w_codes, w_scales = {}, {}, {}, {}
+        for name, cols in (("w1", H), ("w3", H), ("w2", N)):
+            raws[name] = keep.tile([P, PACK, cols], F32, name=name + "_raw", tag=name + "_raw", align_bytes=64)
+            roundeds[name] = keep.tile([P, cols * PACK], BF16, name=name + "_rounded", align_bytes=64)
+            w_scales[name] = keep.tile([P, cols], U8, name=name + "_scales", align_bytes=64)
+        for name in ("w1", "w3"):
+            w_codes[name] = keep.tile([P, H], U32, name=name + "_codes", align_bytes=64)
+        picked, quads, x_codes, x_scales = [], [], [], []
         for s, (a, b) in enumerate(SLICES):
-            late.append(keep.tile([P, 2, b - a], F32, name="late%d" % s, align_bytes=64))
+            early = [keep.tile([P, b - a], F32, name="picked%d_%d" % (s, j), align_bytes=64)[:] for j in range(2)]
+            pair = keep.tile([P, 2, b - a], F32, name="pair%d" % s, align_bytes=64)
+            picked.append((*early, pair[:, 0, :], pair[:, 1, :], pair))
             quads.append(keep.tile([P, b - a, PACK], BF16, name="quads%d" % s, align_bytes=64))
             if s < HELD:
                 x_codes.append(keep.tile([P, b - a], U32, name="x_codes%d" % s, align_bytes=64)[:])
@@ -69,71 +71,75 @@ def tile_picked_pick_glu_gelu_srt_e_kernel(tc, xT, w1, w3, w2, offs, out):
             upto = T - S + b
             nc.sync.dma_start(rows[3][:, done:upto], tokens[:, 3, done:upto])
             done = upto
-        for name in ("w1", "w3", "w2"):
-            nc.sync.dma_start(weights[name][0][:], weights[name][4])
+        for name, src in (("w1", w1), ("w3", w3), ("w2", w2)):
+            nc.sync.dma_start(raws[name][:], src.rearrange("(p j) c -> p j c", j=PACK))
 
-        def entries(s):
+        def window(s, j):
             a, b = SLICES[s]
-            return offsets[:, a // 16 : b // 16]
+            upto = T if j < PACK - 1 else T - S + min(e for e in PIECES if e >= b)
+            return rows[j][:, 0:upto].indirect(offsets[:, a // 16 : b // 16])
 
-        def place_early(s):
-            a, b = SLICES[s]
-            nc.vector.tensor_copy(quads[s][:, :, 0:2], early[:, :, a:b].rearrange("p j n -> p n j"))
+        def gather_scalar(s, j):
+            nc.scalar.activation(picked[s][j], window(s, j), COPY)
 
-        def gather_last(s):
-            nc.scalar.activation(late[s][:, 1, :], rows[3][:, 0 : T - S + min(b for b in PIECES if b >= SLICES[s][1])].indirect(entries(s)), COPY)
+        def gather_vector(s, j):
+            nc.vector.tensor_copy(picked[s][j], window(s, j))
 
-        def place_late(s):
-            nc.vector.tensor_copy(quads[s][:, :, 2:4], late[s][:].rearrange("p j n -> p n j"))
+        def place(s, j):
+            nc.vector.tensor_copy(quads[s][:, :, j], picked[s][j])
+
+        def place_pair(s):
+            nc.vector.tensor_copy(quads[s][:, :, 2:4], picked[s][4][:].rearrange("p j n -> p n j"))
 
         def quantise_x(s):
             nc.vector.quantize_mx(x_codes[s].bitcast(FP8X4), x_scales[s][:], quads[s][:].rearrange("p n j -> p (n j)"))
 
         def dealt(name, lo, hi, t0):
-            raw, rounded = weights[name][0], weights[name][1]
-            return (rounded[:].rearrange("p (t m j) -> p m j t", t=PACK, j=PACK)[:, lo:hi, :, t0 : t0 + 2],
-                    raw[:].rearrange("p j (m t) -> p m j t", t=PACK)[:, lo:hi, :, t0 : t0 + 2])
+            return (roundeds[name][:].rearrange("p (t m j) -> p m j t", t=PACK, j=PACK)[:, lo:hi, :, t0 : t0 + 2],
+                    raws[name][:].rearrange("p j (m t) -> p m j t", t=PACK)[:, lo:hi, :, t0 : t0 + 2])
 
         def quantise_w(name, lo, hi):
-            rounded, codes, scales = weights[name][1:4]
-            nc.vector.quantize_mx(codes[:, lo:hi].bitcast(FP8X4), scales[:, lo:hi], rounded[:, PACK * lo : PACK * hi])
+            nc.vector.quantize_mx(w_codes[name][:, lo:hi].bitcast(FP8X4), w_scales[name][:, lo:hi],
+                                  roundeds[name][:, PACK * lo : PACK * hi])
 
-        def prepare_w(name):
-            share = SCALAR_SHARE[name]
-            if share > P:
-                nc.scalar.copy(*dealt(name, 0, share - P, 2))
-            nc.scalar.copy(*dealt(name, 0, min(share, P), 0))
-            nc.vector.tensor_copy(*dealt(name, max(share - P, 0), P, 2))
-            if share < P:
-                nc.vector.tensor_copy(*dealt(name, share, P, 0))
+        def prepare_w(name, share):
+            for t0 in (2, 0):
+                nc.scalar.copy(*dealt(name, 0, share, t0))
+            for t0 in (2, 0):
+                nc.vector.tensor_copy(*dealt(name, share, P, t0))
             quantise_w(name, H // 2, H)
             quantise_w(name, 0, H // 2)
 
         def round_w2():
-            raw, rounded = weights["w2"][0], weights["w2"][1]
-            nc.vector.tensor_copy(rounded[:].rearrange("p (c i j) -> p c j i", i=2, j=PACK),
-                                  raw[:].rearrange("p j (c i) -> p c j i", i=2))
+            nc.vector.tensor_copy(roundeds["w2"][:].rearrange("p (c i j) -> p c j i", i=2, j=PACK),
+                                  raws["w2"][:].rearrange("p j (c i) -> p c j i", i=2))
 
         def product(bank, name, i):
             s = max(k for k, (a, b) in enumerate(SLICES) if a <= i * BLOCK)
             at = i * BLOCK - SLICES[s][0]
-            codes, scales = weights[name][2], weights[name][3]
             for t in (2, 3, 0, 1):
                 cols = slice(t * P, (t + 1) * P)
                 nc.tensor.matmul_mx(
                     out=bank[:, t, :],
-                    lhsT=codes[:, cols].bitcast(FP8X4), lhsT_scale=scales[:, cols],
+                    lhsT=w_codes[name][:, cols].bitcast(FP8X4), lhsT_scale=w_scales[name][:, cols],
                     rhs=x_codes[s][:, at : at + BLOCK].bitcast(FP8X4), rhs_scale=x_scales[s][:, at : at + BLOCK],
                     start=True, stop=True)
 
         gelus, linears, hiddens = {}, {}, {}
 
+        def woven(bank):
+            return bank[:].rearrange("p t (j c) -> p j c t", j=PACK)
+
         def gate(i):
             bank = gate_banks.tile([P, PACK, BLOCK], F32, name="gate_bank")
             product(bank, "w1", i)
-            if i not in gelus:
-                gelus[i] = keep.tile([P, BLOCK, PACK], F32, name="gelu%d" % i, align_bytes=64)[:]
-            nc.scalar.activation(gelus[i], bank[:].rearrange("p t n -> p n t"), GELU)
+            if i < GELU_LEAD:
+                at = 0 if i == 0 else PACK * W3_SCALAR + (i - 1) * BLOCK
+                gelus[i] = raws["w3"][:, :, at : at + BLOCK].rearrange("p j (c t) -> p j c t", t=PACK)
+            else:
+                own = keep.tile([P, BLOCK * PACK], F32, name="gelu%d" % i, align_bytes=64)
+                gelus[i] = own[:].rearrange("p (j c t) -> p j c t", j=PACK, t=PACK)
+            nc.scalar.activation(gelus[i], woven(bank), GELU)
 
         def linear(i):
             linears[i] = lin_banks.tile([P, PACK, BLOCK], F32, name="lin_bank")
@@ -144,7 +150,8 @@ def tile_picked_pick_glu_gelu_srt_e_kernel(tc, xT, w1, w3, w2, offs, out):
             if i == lo:
                 hiddens[q] = keep.tile([P, (hi - lo) * BLOCK, PACK], BF16, name="hidden%d" % q, align_bytes=64)
             at = (i - lo) * BLOCK
-            nc.vector.tensor_tensor(hiddens[q][:, at : at + BLOCK, :], linears[i][:].rearrange("p t n -> p n t"), gelus[i], MULT)
+            nc.vector.tensor_tensor(hiddens[q][:, at : at + BLOCK, :].rearrange("p (j c) t -> p j c t", j=PACK),
+                                    woven(linears[i]), gelus[i], MULT)
 
         def finish(q):
             lo, hi = GROUPS[q]
@@ -152,13 +159,12 @@ def tile_picked_pick_glu_gelu_srt_e_kernel(tc, xT, w1, w3, w2, offs, out):
             h_codes = keep.tile([P, n], U32, name="h_codes%d" % q, align_bytes=64)
             h_scales = keep.tile([P, n], U8, name="h_scales%d" % q, align_bytes=64)
             nc.vector.quantize_mx(h_codes[:].bitcast(FP8X4), h_scales[:], hiddens[q][:].rearrange("p n t -> p (n t)"))
-            codes, scales = weights["w2"][2], weights["w2"][3]
             y = y_banks.tile([P, N // P, n], F32, name="y_bank")
             for m in range(N // P):
                 cols = slice(m * P, (m + 1) * P)
                 nc.tensor.matmul_mx(
                     out=y[:, m, :],
-                    lhsT=codes[:, cols].bitcast(FP8X4), lhsT_scale=scales[:, cols],
+                    lhsT=w_codes["w2"][:, cols].bitcast(FP8X4), lhsT_scale=w_scales["w2"][:, cols],
                     rhs=h_codes[:].bitcast(FP8X4), rhs_scale=h_scales[:],
                     start=True, stop=True)
             y_out = keep.tile([P, N // P, n], F32, name="y_out%d" % q)
@@ -168,30 +174,34 @@ def tile_picked_pick_glu_gelu_srt_e_kernel(tc, xT, w1, w3, w2, offs, out):
                 nc.scalar.copy(y_out[:], y[:])
             nc.sync.dma_start(out.rearrange("(m p) n -> p m n", p=P)[:, :, lo * BLOCK : hi * BLOCK], y_out[:])
 
-        for j in (0, 1):
-            nc.scalar.activation(early[:, j, :], rows[j][:].indirect(offsets[:]), COPY)
-        for s in range(len(SLICES)):
-            place_early(s)
-        for s in range(HELD):
-            nc.scalar.activation(late[s][:, 0, :], rows[2][:].indirect(entries(s)), COPY)
+        last = len(SLICES) - 1
+        for j in range(2):
+            gather_vector(last, j)
+            for s in range(last):
+                gather_scalar(s, j)
+            for s in (0, last, *range(1, last)):
+                place(s, j)
         for s in range(HELD, len(SLICES)):
-            nc.vector.tensor_copy(late[s][:, 0, :], rows[2][:].indirect(entries(s)))
+            gather_vector(s, 2)
+        for s in range(HELD):
+            gather_scalar(s, 2)
+            place(s, 2)
         for s in range(len(SLICES)):
-            gather_last(s)
-            place_late(s)
+            gather_scalar(s, 3)
+            if s < HELD:
+                place(s, 3)
+            else:
+                place_pair(s)
             if 0 < s <= HELD:
                 quantise_x(s - 1)
-        prepare_w("w1")
-
+        prepare_w("w1", W1_SCALAR)
         held = keep.tile([P, S - SLICES[HELD][0]], U32, name="held", tag="w1_raw", align_bytes=64)
         for s in range(HELD, len(SLICES)):
             x_codes.append(held[:, SLICES[s][0] - SLICES[HELD][0] : SLICES[s][1] - SLICES[HELD][0]])
             quantise_x(s)
-        prepare_w("w3")
+        prepare_w("w3", W3_SCALAR)
         round_w2()
-        first = keep.tile([P, GELU_LEAD * BLOCK, PACK], F32, name="first", tag="w3_raw", align_bytes=64)
         for i in range(GELU_LEAD):
-            gelus[i] = first[:, i * BLOCK : (i + 1) * BLOCK, :]
             gate(i)
         for i in range(LIN_LEAD):
             linear(i)
@@ -204,8 +214,7 @@ def tile_picked_pick_glu_gelu_srt_e_kernel(tc, xT, w1, w3, w2, offs, out):
                     linear(i + LIN_LEAD)
                 multiply(q, i)
                 if i == GELU_LEAD - 1:
-                    w2_codes = keep.tile([P, N], U32, name="w2_codes", tag="w3_raw", align_bytes=64)
-                    weights["w2"][2] = w2_codes
+                    w_codes["w2"] = keep.tile([P, N], U32, name="w2_codes", tag="w3_raw", align_bytes=64)
                     quantise_w("w2", 0, N)
                 if pending is not None:
                     finish(pending)

@@ -21,12 +21,12 @@ BLOCK = 128
 BLOCKS = S // BLOCK
 SLICES = ((0, 128), (128, 384), (384, 640), (640, 896), (896, 1152), (1152, 1536))
 PIECES = (128, 384, 896, 1536)
-HELD = 4
-GROUPS = ((0, 2), (2, 4), (4, 6), (6, 8), (8, 10), (10, 11), (11, 12))
-W1_SCALAR = 96
+GROUPS = ((0, 2), (2, 4), (4, 6), (6, 8), (8, 9), (9, 10), (10, 11), (11, 12))
+W1_SCALAR = 80
 W3_SCALAR = 44
 GELU_LEAD = 3
 LIN_LEAD = 2
+OUT_AFTER = (4, 7, 9, 10, 10, 11, 11, 11)
 
 
 def tile_picked_pick_glu_gelu_srt_e_kernel(tc, xT, w1, w3, w2, offs, out):
@@ -45,17 +45,13 @@ def tile_picked_pick_glu_gelu_srt_e_kernel(tc, xT, w1, w3, w2, offs, out):
         for name, cols in (("w1", H), ("w3", H), ("w2", N)):
             raws[name] = keep.tile([P, PACK, cols], F32, name=name + "_raw", tag=name + "_raw", align_bytes=64)
             roundeds[name] = keep.tile([P, cols * PACK], BF16, name=name + "_rounded", align_bytes=64)
+            w_codes[name] = keep.tile([P, cols], U32, name=name + "_codes", align_bytes=64)
             w_scales[name] = keep.tile([P, cols], U8, name=name + "_scales", align_bytes=64)
-        for name in ("w1", "w3"):
-            w_codes[name] = keep.tile([P, H], U32, name=name + "_codes", align_bytes=64)
         picked, quads, x_codes, x_scales = [], [], [], []
         for s, (a, b) in enumerate(SLICES):
-            early = [keep.tile([P, b - a], F32, name="picked%d_%d" % (s, j), align_bytes=64)[:] for j in range(2)]
-            pair = keep.tile([P, 2, b - a], F32, name="pair%d" % s, align_bytes=64)
-            picked.append((*early, pair[:, 0, :], pair[:, 1, :], pair))
+            picked.append([keep.tile([P, b - a], F32, name="picked%d_%d" % (s, j), align_bytes=64)[:] for j in range(PACK)])
             quads.append(keep.tile([P, b - a, PACK], BF16, name="quads%d" % s, align_bytes=64))
-            if s < HELD:
-                x_codes.append(keep.tile([P, b - a], U32, name="x_codes%d" % s, align_bytes=64)[:])
+            x_codes.append(keep.tile([P, b - a], U32, name="x_codes%d" % s, align_bytes=64)[:])
             x_scales.append(keep.tile([P, b - a], U8, name="x_scales%d" % s, align_bytes=64))
 
         nc.vector.memset(warm[:], 0.0)
@@ -88,9 +84,6 @@ def tile_picked_pick_glu_gelu_srt_e_kernel(tc, xT, w1, w3, w2, offs, out):
         def place(s, j):
             nc.vector.tensor_copy(quads[s][:, :, j], picked[s][j])
 
-        def place_pair(s):
-            nc.vector.tensor_copy(quads[s][:, :, 2:4], picked[s][4][:].rearrange("p j n -> p n j"))
-
         def quantise_x(s):
             nc.vector.quantize_mx(x_codes[s].bitcast(FP8X4), x_scales[s][:], quads[s][:].rearrange("p n j -> p (n j)"))
 
@@ -102,11 +95,13 @@ def tile_picked_pick_glu_gelu_srt_e_kernel(tc, xT, w1, w3, w2, offs, out):
             nc.vector.quantize_mx(w_codes[name][:, lo:hi].bitcast(FP8X4), w_scales[name][:, lo:hi],
                                   roundeds[name][:, PACK * lo : PACK * hi])
 
-        def prepare_w(name, share):
+        def prepare_w(name, share, between=None):
             for t0 in (2, 0):
                 nc.scalar.copy(*dealt(name, 0, share, t0))
             for t0 in (2, 0):
                 nc.vector.tensor_copy(*dealt(name, share, P, t0))
+            if between is not None:
+                quantise_x(between)
             quantise_w(name, H // 2, H)
             quantise_w(name, 0, H // 2)
 
@@ -153,13 +148,24 @@ def tile_picked_pick_glu_gelu_srt_e_kernel(tc, xT, w1, w3, w2, offs, out):
             nc.vector.tensor_tensor(hiddens[q][:, at : at + BLOCK, :].rearrange("p (j c) t -> p j c t", j=PACK),
                                     woven(linears[i]), gelus[i], MULT)
 
-        def finish(q):
+        h_quantised = {}
+
+        def quantise_h(q):
             lo, hi = GROUPS[q]
             n = (hi - lo) * BLOCK
             h_codes = keep.tile([P, n], U32, name="h_codes%d" % q, align_bytes=64)
             h_scales = keep.tile([P, n], U8, name="h_scales%d" % q, align_bytes=64)
             nc.vector.quantize_mx(h_codes[:].bitcast(FP8X4), h_scales[:], hiddens[q][:].rearrange("p n t -> p (n t)"))
-            y = y_banks.tile([P, N // P, n], F32, name="y_bank")
+            h_quantised[q] = (h_codes, h_scales)
+
+        def finish(q):
+            lo, hi = GROUPS[q]
+            n = (hi - lo) * BLOCK
+            h_codes, h_scales = h_quantised[q]
+            if q < len(GROUPS) - 3:
+                y = y_banks.tile([P, N // P, n], F32, name="y_bank")
+            else:
+                y = gate_banks.tile([P, N // P, n], F32, name="gate_bank")
             for m in range(N // P):
                 cols = slice(m * P, (m + 1) * P)
                 nc.tensor.matmul_mx(
@@ -175,49 +181,35 @@ def tile_picked_pick_glu_gelu_srt_e_kernel(tc, xT, w1, w3, w2, offs, out):
             nc.sync.dma_start(out.rearrange("(m p) n -> p m n", p=P)[:, :, lo * BLOCK : hi * BLOCK], y_out[:])
 
         last = len(SLICES) - 1
-        for j in range(2):
+        for j in range(PACK - 1):
             gather_vector(last, j)
             for s in range(last):
                 gather_scalar(s, j)
             for s in (0, last, *range(1, last)):
                 place(s, j)
-        for s in range(HELD, len(SLICES)):
-            gather_vector(s, 2)
-        for s in range(HELD):
-            gather_scalar(s, 2)
-            place(s, 2)
         for s in range(len(SLICES)):
             gather_scalar(s, 3)
-            if s < HELD:
-                place(s, 3)
-            else:
-                place_pair(s)
-            if 0 < s <= HELD:
+            place(s, 3)
+            if s > 0:
                 quantise_x(s - 1)
-        prepare_w("w1", W1_SCALAR)
-        held = keep.tile([P, S - SLICES[HELD][0]], U32, name="held", tag="w1_raw", align_bytes=64)
-        for s in range(HELD, len(SLICES)):
-            x_codes.append(held[:, SLICES[s][0] - SLICES[HELD][0] : SLICES[s][1] - SLICES[HELD][0]])
-            quantise_x(s)
+        prepare_w("w1", W1_SCALAR, last)
         prepare_w("w3", W3_SCALAR)
         round_w2()
-        for i in range(GELU_LEAD):
-            gate(i)
-        for i in range(LIN_LEAD):
-            linear(i)
-        pending = None
-        for q, (lo, hi) in enumerate(GROUPS):
-            for i in range(lo, hi):
-                if i + GELU_LEAD < BLOCKS:
-                    gate(i + GELU_LEAD)
-                if i + LIN_LEAD < BLOCKS:
-                    linear(i + LIN_LEAD)
-                multiply(q, i)
-                if i == GELU_LEAD - 1:
-                    w_codes["w2"] = keep.tile([P, N], U32, name="w2_codes", tag="w3_raw", align_bytes=64)
-                    quantise_w("w2", 0, N)
-                if pending is not None:
-                    finish(pending)
-                    pending = None
-            pending = q
-        finish(pending)
+        quantise_w("w2", 0, N)
+        gate(0)
+        gate(1)
+        linear(0)
+        gate(2)
+        linear(1)
+        for i in range(BLOCKS):
+            if i + GELU_LEAD < BLOCKS:
+                gate(i + GELU_LEAD)
+            if i + LIN_LEAD < BLOCKS:
+                linear(i + LIN_LEAD)
+            multiply(max(q for q, (lo, hi) in enumerate(GROUPS) if lo <= i), i)
+            for q, (lo, hi) in enumerate(GROUPS):
+                if hi == i or (hi == BLOCKS and i == BLOCKS - 1):
+                    quantise_h(q)
+            for q in range(len(GROUPS)):
+                if OUT_AFTER[q] == i:
+                    finish(q)

@@ -22,11 +22,13 @@ BLOCKS = S // BLOCK
 SLICES = ((0, 128), (128, 384), (384, 640), (640, 896), (896, 1152), (1152, 1536))
 PIECES = (128, 384, 896, 1536)
 GROUPS = ((0, 2), (2, 4), (4, 6), (6, 8), (8, 9), (9, 10), (10, 11), (11, 12))
-W1_SCALAR = 80
-W3_SCALAR = 44
+W1_SCALAR = 128
+W3_SCALAR = 64
 GELU_LEAD = 3
 LIN_LEAD = 2
 OUT_AFTER = (4, 7, 9, 10, 10, 11, 11, 11)
+EARLY_VECTOR = 4
+HELD = 5
 
 
 def tile_picked_pick_glu_gelu_srt_e_kernel(tc, xT, w1, w3, w2, offs, out):
@@ -44,14 +46,15 @@ def tile_picked_pick_glu_gelu_srt_e_kernel(tc, xT, w1, w3, w2, offs, out):
         raws, roundeds, w_codes, w_scales = {}, {}, {}, {}
         for name, cols in (("w1", H), ("w3", H), ("w2", N)):
             raws[name] = keep.tile([P, PACK, cols], F32, name=name + "_raw", tag=name + "_raw", align_bytes=64)
-            roundeds[name] = keep.tile([P, cols * PACK], BF16, name=name + "_rounded", align_bytes=64)
+            roundeds[name] = keep.tile([P, cols * PACK], BF16, name=name + "_rounded", tag=name + "_rounded", align_bytes=64)
             w_codes[name] = keep.tile([P, cols], U32, name=name + "_codes", align_bytes=64)
             w_scales[name] = keep.tile([P, cols], U8, name=name + "_scales", align_bytes=64)
         picked, quads, x_codes, x_scales = [], [], [], []
         for s, (a, b) in enumerate(SLICES):
-            picked.append([keep.tile([P, b - a], F32, name="picked%d_%d" % (s, j), align_bytes=64)[:] for j in range(PACK)])
+            picked.append(keep.tile([P, PACK, b - a], F32, name="picked%d" % s, align_bytes=64))
             quads.append(keep.tile([P, b - a, PACK], BF16, name="quads%d" % s, align_bytes=64))
-            x_codes.append(keep.tile([P, b - a], U32, name="x_codes%d" % s, align_bytes=64)[:])
+            if s < HELD:
+                x_codes.append(keep.tile([P, b - a], U32, name="x_codes%d" % s, align_bytes=64)[:])
             x_scales.append(keep.tile([P, b - a], U8, name="x_scales%d" % s, align_bytes=64))
 
         nc.vector.memset(warm[:], 0.0)
@@ -76,13 +79,14 @@ def tile_picked_pick_glu_gelu_srt_e_kernel(tc, xT, w1, w3, w2, offs, out):
             return rows[j][:, 0:upto].indirect(offsets[:, a // 16 : b // 16])
 
         def gather_scalar(s, j):
-            nc.scalar.activation(picked[s][j], window(s, j), COPY)
+            nc.scalar.activation(picked[s][:, j, :], window(s, j), COPY)
 
         def gather_vector(s, j):
-            nc.vector.tensor_copy(picked[s][j], window(s, j))
+            nc.vector.tensor_copy(picked[s][:, j, :], window(s, j))
 
-        def place(s, j):
-            nc.vector.tensor_copy(quads[s][:, :, j], picked[s][j])
+        def weave(s):
+            nc.vector.tensor_copy(quads[s][:].rearrange("p (c i) j -> p c j i", i=2),
+                                  picked[s][:].rearrange("p j (c i) -> p c j i", i=2))
 
         def quantise_x(s):
             nc.vector.quantize_mx(x_codes[s].bitcast(FP8X4), x_scales[s][:], quads[s][:].rearrange("p n j -> p (n j)"))
@@ -95,13 +99,11 @@ def tile_picked_pick_glu_gelu_srt_e_kernel(tc, xT, w1, w3, w2, offs, out):
             nc.vector.quantize_mx(w_codes[name][:, lo:hi].bitcast(FP8X4), w_scales[name][:, lo:hi],
                                   roundeds[name][:, PACK * lo : PACK * hi])
 
-        def prepare_w(name, share, between=None):
+        def prepare_w(name, share):
             for t0 in (2, 0):
                 nc.scalar.copy(*dealt(name, 0, share, t0))
-            for t0 in (2, 0):
+            for t0 in (2, 0) if share < P else ():
                 nc.vector.tensor_copy(*dealt(name, share, P, t0))
-            if between is not None:
-                quantise_x(between)
             quantise_w(name, H // 2, H)
             quantise_w(name, 0, H // 2)
 
@@ -180,20 +182,23 @@ def tile_picked_pick_glu_gelu_srt_e_kernel(tc, xT, w1, w3, w2, offs, out):
                 nc.scalar.copy(y_out[:], y[:])
             nc.sync.dma_start(out.rearrange("(m p) n -> p m n", p=P)[:, :, lo * BLOCK : hi * BLOCK], y_out[:])
 
-        last = len(SLICES) - 1
         for j in range(PACK - 1):
-            gather_vector(last, j)
-            for s in range(last):
+            for s in range(EARLY_VECTOR):
                 gather_scalar(s, j)
-            for s in (0, last, *range(1, last)):
-                place(s, j)
+            for s in range(EARLY_VECTOR, len(SLICES)):
+                gather_vector(s, j)
         for s in range(len(SLICES)):
             gather_scalar(s, 3)
-            place(s, 3)
-            if s > 0:
+        for s in range(len(SLICES)):
+            weave(s)
+            if 0 < s <= HELD:
                 quantise_x(s - 1)
-        prepare_w("w1", W1_SCALAR, last)
+        prepare_w("w1", W1_SCALAR)
         prepare_w("w3", W3_SCALAR)
+        held = keep.tile([P, S - SLICES[HELD][0]], U32, name="held", tag="w3_rounded", align_bytes=64)
+        for s in range(HELD, len(SLICES)):
+            x_codes.append(held[:, SLICES[s][0] - SLICES[HELD][0] : SLICES[s][1] - SLICES[HELD][0]])
+            quantise_x(s)
         round_w2()
         quantise_w("w2", 0, N)
         gate(0)

@@ -14,21 +14,22 @@ FP8X4 = mybir.dt.float8_e4m3fn_x4
 GELU = mybir.ActivationFunctionType.Gelu_apprx_tanh
 COPY = mybir.ActivationFunctionType.Copy
 MULT = mybir.AluOpType.mult
+ADD = mybir.AluOpType.add
 
 P = 128
 PACK = 4
 BLOCK = 128
 BLOCKS = S // BLOCK
-SLICES = ((0, 128), (128, 384), (384, 640), (640, 896), (896, 1152), (1152, 1536))
-PIECES = (128, 384, 896, 1536)
+SLICES = ((0, 384), (384, 640), (640, 896), (896, 1152), (1152, 1536))
+PIECES = (384, 640, 1024, 1536)
 GROUPS = ((0, 2), (2, 4), (4, 6), (6, 8), (8, 9), (9, 10), (10, 11), (11, 12))
-W1_SCALAR = 128
-W3_SCALAR = 64
+W1_SCALAR = 96
+W3_SCALAR = 52
 GELU_LEAD = 3
 LIN_LEAD = 2
 OUT_AFTER = (4, 7, 9, 10, 10, 11, 11, 11)
-EARLY_VECTOR = 4
-HELD = 5
+EARLY_VECTOR = 0
+WARM_UPS = 5
 
 
 def tile_picked_pick_glu_gelu_srt_e_kernel(tc, xT, w1, w3, w2, offs, out):
@@ -46,15 +47,17 @@ def tile_picked_pick_glu_gelu_srt_e_kernel(tc, xT, w1, w3, w2, offs, out):
         raws, roundeds, w_codes, w_scales = {}, {}, {}, {}
         for name, cols in (("w1", H), ("w3", H), ("w2", N)):
             raws[name] = keep.tile([P, PACK, cols], F32, name=name + "_raw", tag=name + "_raw", align_bytes=64)
-            roundeds[name] = keep.tile([P, cols * PACK], BF16, name=name + "_rounded", tag=name + "_rounded", align_bytes=64)
             w_codes[name] = keep.tile([P, cols], U32, name=name + "_codes", align_bytes=64)
             w_scales[name] = keep.tile([P, cols], U8, name=name + "_scales", align_bytes=64)
+        for name in ("w1", "w3"):
+            for t0 in (0, 2):
+                tag = "%s_rounded%d" % (name, t0)
+                roundeds[name, t0] = keep.tile([P, H * PACK // 2], BF16, name=tag, tag=tag, align_bytes=64)
         picked, quads, x_codes, x_scales = [], [], [], []
         for s, (a, b) in enumerate(SLICES):
             picked.append(keep.tile([P, PACK, b - a], F32, name="picked%d" % s, align_bytes=64))
-            quads.append(keep.tile([P, b - a, PACK], BF16, name="quads%d" % s, align_bytes=64))
-            if s < HELD:
-                x_codes.append(keep.tile([P, b - a], U32, name="x_codes%d" % s, align_bytes=64)[:])
+            quads.append(keep.tile([P, b - a, PACK], BF16, name="quads%d" % s, tag="quads%d" % s, align_bytes=64))
+            x_codes.append(keep.tile([P, b - a], U32, name="x_codes%d" % s, align_bytes=64)[:] if s < len(SLICES) - 1 else None)
             x_scales.append(keep.tile([P, b - a], U8, name="x_scales%d" % s, align_bytes=64))
 
         nc.vector.memset(warm[:], 0.0)
@@ -88,16 +91,21 @@ def tile_picked_pick_glu_gelu_srt_e_kernel(tc, xT, w1, w3, w2, offs, out):
             nc.vector.tensor_copy(quads[s][:].rearrange("p (c i) j -> p c j i", i=2),
                                   picked[s][:].rearrange("p j (c i) -> p c j i", i=2))
 
+        def place(s, j):
+            nc.vector.tensor_copy(quads[s][:, :, j], picked[s][:, j, :])
+
         def quantise_x(s):
+            if s == len(SLICES) - 1:
+                x_codes[s] = keep.tile([P, S - SLICES[s][0]], U32, name="x_codes_last", tag="w3_rounded2", align_bytes=64)[:]
             nc.vector.quantize_mx(x_codes[s].bitcast(FP8X4), x_scales[s][:], quads[s][:].rearrange("p n j -> p (n j)"))
 
         def dealt(name, lo, hi, t0):
-            return (roundeds[name][:].rearrange("p (t m j) -> p m j t", t=PACK, j=PACK)[:, lo:hi, :, t0 : t0 + 2],
+            return (roundeds[name, t0][:].rearrange("p (t m j) -> p m j t", t=2, j=PACK)[:, lo:hi],
                     raws[name][:].rearrange("p j (m t) -> p m j t", t=PACK)[:, lo:hi, :, t0 : t0 + 2])
 
         def quantise_w(name, lo, hi):
             nc.vector.quantize_mx(w_codes[name][:, lo:hi].bitcast(FP8X4), w_scales[name][:, lo:hi],
-                                  roundeds[name][:, PACK * lo : PACK * hi])
+                                  roundeds[name, lo // P][:])
 
         def prepare_w(name, share):
             for t0 in (2, 0):
@@ -108,8 +116,14 @@ def tile_picked_pick_glu_gelu_srt_e_kernel(tc, xT, w1, w3, w2, offs, out):
             quantise_w(name, 0, H // 2)
 
         def round_w2():
-            nc.vector.tensor_copy(roundeds["w2"][:].rearrange("p (c i j) -> p c j i", i=2, j=PACK),
+            roundeds["w2", 0] = keep.tile([P, N * PACK], BF16, name="w2_rounded", tag="w3_rounded0", align_bytes=64)
+            nc.vector.tensor_copy(roundeds["w2", 0][:].rearrange("p (c i j) -> p c j i", i=2, j=PACK),
                                   raws["w2"][:].rearrange("p j (c i) -> p c j i", i=2))
+
+        def round_w2_gpsimd(tag):
+            roundeds["w2", 0] = keep.tile([P, N * PACK], BF16, name="w2_rounded_late", tag=tag, align_bytes=64)
+            nc.gpsimd.tensor_scalar(roundeds["w2", 0][:].rearrange("p (c j) -> p c j", j=PACK),
+                                    raws["w2"][:].rearrange("p j c -> p c j"), 1.0, 0.0, MULT, ADD)
 
         def product(bank, name, i):
             s = max(k for k, (a, b) in enumerate(SLICES) if a <= i * BLOCK)
@@ -121,6 +135,21 @@ def tile_picked_pick_glu_gelu_srt_e_kernel(tc, xT, w1, w3, w2, offs, out):
                     lhsT=w_codes[name][:, cols].bitcast(FP8X4), lhsT_scale=w_scales[name][:, cols],
                     rhs=x_codes[s][:, at : at + BLOCK].bitcast(FP8X4), rhs_scale=x_scales[s][:, at : at + BLOCK],
                     start=True, stop=True)
+
+        def warm_up(s):
+            idle = y_banks.tile([P, N // P, 2 * BLOCK], F32, name="y_bank")
+            for k in range(WARM_UPS):
+                nc.tensor.matmul_mx(
+                    out=idle[:, k % 2, :],
+                    lhsT=x_codes[s][:, 0:P].bitcast(FP8X4), lhsT_scale=x_scales[s][:, 0:P],
+                    rhs=x_codes[s][:, 0 : 2 * BLOCK].bitcast(FP8X4), rhs_scale=x_scales[s][:, 0 : 2 * BLOCK],
+                    start=True, stop=True)
+
+        def round_w(name, share, t0, engine):
+            if engine == "s":
+                nc.scalar.copy(*dealt(name, 0, share, t0))
+            elif share < P:
+                nc.vector.tensor_copy(*dealt(name, share, P, t0))
 
         gelus, linears, hiddens = {}, {}, {}
 
@@ -142,7 +171,8 @@ def tile_picked_pick_glu_gelu_srt_e_kernel(tc, xT, w1, w3, w2, offs, out):
             linears[i] = lin_banks.tile([P, PACK, BLOCK], F32, name="lin_bank")
             product(linears[i], "w3", i)
 
-        def multiply(q, i):
+        def multiply(i):
+            q = max(k for k, (lo, hi) in enumerate(GROUPS) if lo <= i)
             lo, hi = GROUPS[q]
             if i == lo:
                 hiddens[q] = keep.tile([P, (hi - lo) * BLOCK, PACK], BF16, name="hidden%d" % q, align_bytes=64)
@@ -164,6 +194,19 @@ def tile_picked_pick_glu_gelu_srt_e_kernel(tc, xT, w1, w3, w2, offs, out):
             lo, hi = GROUPS[q]
             n = (hi - lo) * BLOCK
             h_codes, h_scales = h_quantised[q]
+            if n == 4 * BLOCK:
+                for m in range(N // P):
+                    cols = slice(m * P, (m + 1) * P)
+                    y = y_banks.tile([P, n], F32, name="y_bank")
+                    nc.tensor.matmul_mx(
+                        out=y[:],
+                        lhsT=w_codes["w2"][:, cols].bitcast(FP8X4), lhsT_scale=w_scales["w2"][:, cols],
+                        rhs=h_codes[:].bitcast(FP8X4), rhs_scale=h_scales[:],
+                        start=True, stop=True)
+                    y_out = keep.tile([P, n], F32, name="y_out%d_%d" % (q, m))
+                    nc.scalar.copy(y_out[:], y[:])
+                    nc.sync.dma_start(out[cols, lo * BLOCK : hi * BLOCK], y_out[:])
+                return
             if q < len(GROUPS) - 3:
                 y = y_banks.tile([P, N // P, n], F32, name="y_bank")
             else:
@@ -187,34 +230,85 @@ def tile_picked_pick_glu_gelu_srt_e_kernel(tc, xT, w1, w3, w2, offs, out):
                 gather_scalar(s, j)
             for s in range(EARLY_VECTOR, len(SLICES)):
                 gather_vector(s, j)
-        for s in range(len(SLICES)):
-            gather_scalar(s, 3)
-        for s in range(len(SLICES)):
-            weave(s)
-            if 0 < s <= HELD:
-                quantise_x(s - 1)
-        prepare_w("w1", W1_SCALAR)
-        prepare_w("w3", W3_SCALAR)
-        held = keep.tile([P, S - SLICES[HELD][0]], U32, name="held", tag="w3_rounded", align_bytes=64)
-        for s in range(HELD, len(SLICES)):
-            x_codes.append(held[:, SLICES[s][0] - SLICES[HELD][0] : SLICES[s][1] - SLICES[HELD][0]])
-            quantise_x(s)
+        gather_vector(0, 3)
+        gather_scalar(1, 3)
+        gather_scalar(2, 3)
+        gather_scalar(3, 3)
+        gather_scalar(4, 3)
+        weave(0)
+        weave(1)
+        quantise_x(0)
+        quantise_x(1)
+        weave(2)
+        weave(3)
+        quantise_x(2)
+        warm_up(2)
+        weave(4)
+        round_w("w1", W1_SCALAR, 2, "s")
+        round_w("w1", W1_SCALAR, 0, "s")
+        round_w("w1", W1_SCALAR, 2, "v")
+        round_w("w1", W1_SCALAR, 0, "v")
+        quantise_w("w1", H // 2, H)
+        quantise_x(3)
+        quantise_w("w1", 0, H // 2)
+        round_w("w3", W3_SCALAR, 2, "s")
+        round_w("w3", W3_SCALAR, 0, "s")
+        round_w("w3", W3_SCALAR, 2, "v")
+        round_w("w3", W3_SCALAR, 0, "v")
+        quantise_w("w3", H // 2, H)
+        quantise_w("w3", 0, H // 2)
+        quantise_x(4)
         round_w2()
-        quantise_w("w2", 0, N)
         gate(0)
         gate(1)
         linear(0)
         gate(2)
         linear(1)
-        for i in range(BLOCKS):
-            if i + GELU_LEAD < BLOCKS:
-                gate(i + GELU_LEAD)
-            if i + LIN_LEAD < BLOCKS:
-                linear(i + LIN_LEAD)
-            multiply(max(q for q, (lo, hi) in enumerate(GROUPS) if lo <= i), i)
-            for q, (lo, hi) in enumerate(GROUPS):
-                if hi == i or (hi == BLOCKS and i == BLOCKS - 1):
-                    quantise_h(q)
-            for q in range(len(GROUPS)):
-                if OUT_AFTER[q] == i:
-                    finish(q)
+        gate(3)
+        linear(2)
+        multiply(0)
+        quantise_w("w2", 0, N)
+        gate(4)
+        linear(3)
+        multiply(1)
+        gate(5)
+        linear(4)
+        multiply(2)
+        quantise_h(0)
+        gate(6)
+        linear(5)
+        multiply(3)
+        finish(0)
+        gate(7)
+        linear(6)
+        multiply(4)
+        quantise_h(1)
+        gate(8)
+        linear(7)
+        multiply(5)
+        finish(1)
+        gate(9)
+        linear(8)
+        multiply(6)
+        quantise_h(2)
+        gate(10)
+        linear(9)
+        multiply(7)
+        finish(2)
+        gate(11)
+        linear(10)
+        multiply(8)
+        quantise_h(3)
+        linear(11)
+        finish(3)
+        multiply(9)
+        quantise_h(4)
+        finish(4)
+        multiply(10)
+        quantise_h(5)
+        finish(5)
+        multiply(11)
+        quantise_h(6)
+        quantise_h(7)
+        finish(6)
+        finish(7)

@@ -21,9 +21,9 @@ PACK = 4
 BLOCK = 128
 BLOCKS = S // BLOCK
 SLICES = ((0, 384), (384, 640), (640, 896), (896, 1152), (1152, 1536))
-PIECES = (384, 640, 1024, 1536)
-GROUPS = ((0, 2), (2, 4), (4, 6), (6, 8), (8, 9), (9, 10), (10, 11), (11, 12))
-W1_SCALAR = 96
+PIECES = (384, 640, 1536)
+GROUPS = ((0, 4), (4, 6), (6, 8), (8, 9), (9, 10), (10, 11), (11, 12))
+W1_SCALAR = 104
 W3_SCALAR = 52
 GELU_LEAD = 3
 LIN_LEAD = 2
@@ -145,6 +145,14 @@ def tile_picked_pick_glu_gelu_srt_e_kernel(tc, xT, w1, w3, w2, offs, out):
                     rhs=x_codes[s][:, 0 : 2 * BLOCK].bitcast(FP8X4), rhs_scale=x_scales[s][:, 0 : 2 * BLOCK],
                     start=True, stop=True)
 
+        def prepare_w1():
+            rounded = keep.tile([P, H * PACK], BF16, name="w1_rounded", align_bytes=64)
+            dst = rounded[:].rearrange("p (t m j) -> p m j t", t=PACK, j=PACK)
+            src = raws["w1"][:].rearrange("p j (m t) -> p m j t", t=PACK)
+            nc.scalar.copy(dst[:, 0:W1_SCALAR], src[:, 0:W1_SCALAR])
+            nc.vector.tensor_copy(dst[:, W1_SCALAR:P], src[:, W1_SCALAR:P])
+            return rounded
+
         def round_w(name, share, t0, engine):
             if engine == "s":
                 nc.scalar.copy(*dealt(name, 0, share, t0))
@@ -258,7 +266,7 @@ def tile_picked_pick_glu_gelu_srt_e_kernel(tc, xT, w1, w3, w2, offs, out):
         quantise_w("w3", H // 2, H)
         quantise_w("w3", 0, H // 2)
         quantise_x(4)
-        round_w2()
+        round_w2_gpsimd("quads4")
         gate(0)
         gate(1)
         linear(0)
@@ -267,48 +275,46 @@ def tile_picked_pick_glu_gelu_srt_e_kernel(tc, xT, w1, w3, w2, offs, out):
         gate(3)
         linear(2)
         multiply(0)
-        quantise_w("w2", 0, N)
         gate(4)
         linear(3)
         multiply(1)
         gate(5)
         linear(4)
         multiply(2)
-        quantise_h(0)
         gate(6)
         linear(5)
         multiply(3)
-        finish(0)
+        quantise_h(0)
+        quantise_w("w2", 0, N)
         gate(7)
         linear(6)
         multiply(4)
-        quantise_h(1)
+        finish(0)
         gate(8)
         linear(7)
         multiply(5)
-        finish(1)
         gate(9)
         linear(8)
         multiply(6)
-        quantise_h(2)
+        quantise_h(1)
         gate(10)
         linear(9)
         multiply(7)
-        finish(2)
+        finish(1)
         gate(11)
         linear(10)
         multiply(8)
-        quantise_h(3)
+        quantise_h(2)
         linear(11)
-        finish(3)
+        finish(2)
         multiply(9)
+        quantise_h(3)
+        finish(3)
+        multiply(10)
         quantise_h(4)
         finish(4)
-        multiply(10)
-        quantise_h(5)
-        finish(5)
         multiply(11)
+        quantise_h(5)
         quantise_h(6)
-        quantise_h(7)
+        finish(5)
         finish(6)
-        finish(7)

@@ -24,11 +24,11 @@ SLICES = ((0, 384), (384, 640), (640, 896), (896, 1152), (1152, 1536))
 PIECES = (384, 640, 1536)
 GROUPS = ((0, 4), (4, 6), (6, 8), (8, 9), (9, 10), (10, 11), (11, 12))
 W1_SCALAR = 104
-W3_SCALAR = 52
+W3_SCALAR = 64
 GELU_LEAD = 3
 LIN_LEAD = 2
 OUT_AFTER = (4, 7, 9, 10, 10, 11, 11, 11)
-EARLY_VECTOR = 0
+EARLY_VECTOR = 2
 WARM_UPS = 5
 
 
@@ -57,7 +57,7 @@ def tile_picked_pick_glu_gelu_srt_e_kernel(tc, xT, w1, w3, w2, offs, out):
         for s, (a, b) in enumerate(SLICES):
             picked.append(keep.tile([P, PACK, b - a], F32, name="picked%d" % s, align_bytes=64))
             quads.append(keep.tile([P, b - a, PACK], BF16, name="quads%d" % s, tag="quads%d" % s, align_bytes=64))
-            x_codes.append(keep.tile([P, b - a], U32, name="x_codes%d" % s, align_bytes=64)[:] if s < len(SLICES) - 1 else None)
+            x_codes.append(keep.tile([P, b - a], U32, name="x_codes%d" % s, align_bytes=64)[:] if s < len(SLICES) - 2 else None)
             x_scales.append(keep.tile([P, b - a], U8, name="x_scales%d" % s, align_bytes=64))
 
         nc.vector.memset(warm[:], 0.0)
@@ -95,8 +95,9 @@ def tile_picked_pick_glu_gelu_srt_e_kernel(tc, xT, w1, w3, w2, offs, out):
             nc.vector.tensor_copy(quads[s][:, :, j], picked[s][:, j, :])
 
         def quantise_x(s):
-            if s == len(SLICES) - 1:
-                x_codes[s] = keep.tile([P, S - SLICES[s][0]], U32, name="x_codes_last", tag="w3_rounded2", align_bytes=64)[:]
+            if s >= len(SLICES) - 2:
+                tag = "w3_rounded2" if s == len(SLICES) - 2 else "w3_rounded0"
+                x_codes[s] = keep.tile([P, SLICES[s][1] - SLICES[s][0]], U32, name="x_codes%d" % s, tag=tag, align_bytes=64)[:]
             nc.vector.quantize_mx(x_codes[s].bitcast(FP8X4), x_scales[s][:], quads[s][:].rearrange("p n j -> p (n j)"))
 
         def dealt(name, lo, hi, t0):
@@ -257,7 +258,6 @@ def tile_picked_pick_glu_gelu_srt_e_kernel(tc, xT, w1, w3, w2, offs, out):
         round_w("w1", W1_SCALAR, 2, "v")
         round_w("w1", W1_SCALAR, 0, "v")
         quantise_w("w1", H // 2, H)
-        quantise_x(3)
         quantise_w("w1", 0, H // 2)
         round_w("w3", W3_SCALAR, 2, "s")
         round_w("w3", W3_SCALAR, 0, "s")
@@ -265,6 +265,7 @@ def tile_picked_pick_glu_gelu_srt_e_kernel(tc, xT, w1, w3, w2, offs, out):
         round_w("w3", W3_SCALAR, 0, "v")
         quantise_w("w3", H // 2, H)
         quantise_w("w3", 0, H // 2)
+        quantise_x(3)
         quantise_x(4)
         round_w2_gpsimd("quads4")
         gate(0)
@@ -284,11 +285,11 @@ def tile_picked_pick_glu_gelu_srt_e_kernel(tc, xT, w1, w3, w2, offs, out):
         gate(6)
         linear(5)
         multiply(3)
-        quantise_h(0)
-        quantise_w("w2", 0, N)
         gate(7)
         linear(6)
         multiply(4)
+        quantise_h(0)
+        quantise_w("w2", 0, N)
         finish(0)
         gate(8)
         linear(7)

@@ -24,8 +24,11 @@ SLICES = ((0, 384), (384, 640), (640, 896), (896, 1152), (1152, 1536))
 PIECES = (384, 640, 1536)
 GROUPS = ((0, 4), (4, 6), (6, 8), (8, 9), (9, 10), (10, 11), (11, 12))
 W1_SCALAR = 104
-W3_SCALAR = 64
+W3_SCALAR = 52
 GELU_LEAD = 3
+FREE_GELUS = 1
+VECTOR_RESULTS = 2
+LAST_TAG = "w1_rounded2"
 LIN_LEAD = 2
 OUT_AFTER = (4, 7, 9, 10, 10, 11, 11, 11)
 EARLY_VECTOR = 2
@@ -56,7 +59,7 @@ def tile_picked_pick_glu_gelu_srt_e_kernel(tc, xT, w1, w3, w2, offs, out):
         picked, quads, x_codes, x_scales = [], [], [], []
         for s, (a, b) in enumerate(SLICES):
             picked.append(keep.tile([P, PACK, b - a], F32, name="picked%d" % s, align_bytes=64))
-            quads.append(keep.tile([P, b - a, PACK], BF16, name="quads%d" % s, tag="quads%d" % s, align_bytes=64))
+            quads.append(None if s == len(SLICES) - 1 else keep.tile([P, b - a, PACK], BF16, name="quads%d" % s, tag="quads%d" % s if s < len(SLICES) - 1 else LAST_TAG, align_bytes=64))
             x_codes.append(keep.tile([P, b - a], U32, name="x_codes%d" % s, align_bytes=64)[:] if s < len(SLICES) - 2 else None)
             x_scales.append(keep.tile([P, b - a], U8, name="x_scales%d" % s, align_bytes=64))
 
@@ -88,6 +91,8 @@ def tile_picked_pick_glu_gelu_srt_e_kernel(tc, xT, w1, w3, w2, offs, out):
             nc.vector.tensor_copy(picked[s][:, j, :], window(s, j))
 
         def weave(s):
+            if s == len(SLICES) - 1:
+                quads[s] = keep.tile([P, S - SLICES[s][0], PACK], BF16, name="quads_last", tag=LAST_TAG, align_bytes=64)
             nc.vector.tensor_copy(quads[s][:].rearrange("p (c i) j -> p c j i", i=2),
                                   picked[s][:].rearrange("p j (c i) -> p c j i", i=2))
 
@@ -122,7 +127,7 @@ def tile_picked_pick_glu_gelu_srt_e_kernel(tc, xT, w1, w3, w2, offs, out):
                                   raws["w2"][:].rearrange("p j (c i) -> p c j i", i=2))
 
         def round_w2_gpsimd(tag):
-            roundeds["w2", 0] = keep.tile([P, N * PACK], BF16, name="w2_rounded_late", tag=tag, align_bytes=64)
+            roundeds["w2", 0] = keep.tile([P, N * PACK], BF16, name="w2_rounded_late", tag=LAST_TAG, align_bytes=64)
             nc.gpsimd.tensor_scalar(roundeds["w2", 0][:].rearrange("p (c j) -> p c j", j=PACK),
                                     raws["w2"][:].rearrange("p j c -> p c j"), 1.0, 0.0, MULT, ADD)
 
@@ -168,8 +173,8 @@ def tile_picked_pick_glu_gelu_srt_e_kernel(tc, xT, w1, w3, w2, offs, out):
         def gate(i):
             bank = gate_banks.tile([P, PACK, BLOCK], F32, name="gate_bank")
             product(bank, "w1", i)
-            if i < GELU_LEAD:
-                at = 0 if i == 0 else PACK * W3_SCALAR + (i - 1) * BLOCK
+            if FREE_GELUS <= i < GELU_LEAD:
+                at = (i - FREE_GELUS) * BLOCK
                 gelus[i] = raws["w3"][:, :, at : at + BLOCK].rearrange("p j (c t) -> p j c t", t=PACK)
             else:
                 own = keep.tile([P, BLOCK * PACK], F32, name="gelu%d" % i, align_bytes=64)
@@ -228,7 +233,7 @@ def tile_picked_pick_glu_gelu_srt_e_kernel(tc, xT, w1, w3, w2, offs, out):
                     rhs=h_codes[:].bitcast(FP8X4), rhs_scale=h_scales[:],
                     start=True, stop=True)
             y_out = keep.tile([P, N // P, n], F32, name="y_out%d" % q)
-            if q == len(GROUPS) - 1:
+            if q >= len(GROUPS) - VECTOR_RESULTS:
                 nc.vector.tensor_copy(y_out[:], y[:])
             else:
                 nc.scalar.copy(y_out[:], y[:])
@@ -252,13 +257,13 @@ def tile_picked_pick_glu_gelu_srt_e_kernel(tc, xT, w1, w3, w2, offs, out):
         weave(3)
         quantise_x(2)
         warm_up(2)
-        weave(4)
         round_w("w1", W1_SCALAR, 2, "s")
         round_w("w1", W1_SCALAR, 0, "s")
         round_w("w1", W1_SCALAR, 2, "v")
         round_w("w1", W1_SCALAR, 0, "v")
         quantise_w("w1", H // 2, H)
         quantise_w("w1", 0, H // 2)
+        weave(4)
         round_w("w3", W3_SCALAR, 2, "s")
         round_w("w3", W3_SCALAR, 0, "s")
         round_w("w3", W3_SCALAR, 2, "v")

from contextlib import ExitStack

import concourse.mybir as mybir

K, T, S, H, N = 512, 4096, 1536, 512, 256
FLOPS = 2 * S * (2 * K * H + H * N)

F32 = mybir.dt.float32
BF16 = mybir.dt.bfloat16
U32 = mybir.dt.uint32
U16 = mybir.dt.uint16
U8 = mybir.dt.uint8
FP8X4 = mybir.dt.float8_e4m3fn_x4
GELU = mybir.ActivationFunctionType.Gelu_apprx_tanh
COPY = mybir.ActivationFunctionType.Copy
MULT = mybir.AluOpType.mult
ADD = mybir.AluOpType.add

P = 128
PACK = 4
BLOCK = 128
BLOCKS = S // BLOCK
SLICES = ((0, 384), (384, 640), (640, 896), (896, 1152), (1152, 1536))
PIECES = (384, 640, 1536)
GROUPS = ((0, 4), (4, 6), (6, 8), (8, 9), (9, 10), (10, 11), (11, 12))
W1_SCALAR = 104
W3_SCALAR = 52
GELU_LEAD = 3
FREE_GELUS = 1
VECTOR_RESULTS = 2
LAST_TAG = "w1_rounded2"
LIN_LEAD = 2
OUT_AFTER = (4, 7, 9, 10, 10, 11, 11, 11)
EARLY_VECTOR = 2
WARM_UPS = 5


def tile_picked_pick_glu_gelu_srt_e_kernel(tc, xT, w1, w3, w2, offs, out):
    nc = tc.nc

    with ExitStack() as ctx:
        keep = ctx.enter_context(tc.tile_pool(name="keep", bufs=1))
        gate_banks = ctx.enter_context(tc.psum_pool(name="gate_banks", bufs=3))
        lin_banks = ctx.enter_context(tc.psum_pool(name="lin_banks", bufs=3))
        y_banks = ctx.enter_context(tc.psum_pool(name="y_banks", bufs=2))

        offsets = keep.tile([P, S // 16], U16, name="offsets")
        warm = keep.tile([P, 2], F32, name="warm")
        rows = [keep.tile([P, T], F32, name="row%d" % j, align_bytes=64) for j in range(PACK)]
        raws, roundeds, w_codes, w_scales = {}, {}, {}, {}
        for name, cols in (("w1", H), ("w3", H), ("w2", N)):
            raws[name] = keep.tile([P, PACK, cols], F32, name=name + "_raw", tag=name + "_raw", align_bytes=64)
            w_codes[name] = keep.tile([P, cols], U32, name=name + "_codes", align_bytes=64)
            w_scales[name] = keep.tile([P, cols], U8, name=name + "_scales", align_bytes=64)
        for name in ("w1", "w3"):
            for t0 in (0, 2):
                tag = "%s_rounded%d" % (name, t0)
                roundeds[name, t0] = keep.tile([P, H * PACK // 2], BF16, name=tag, tag=tag, align_bytes=64)
        picked, quads, x_codes, x_scales = [], [], [], []
        for s, (a, b) in enumerate(SLICES):
            picked.append(keep.tile([P, PACK, b - a], F32, name="picked%d" % s, align_bytes=64))
            quads.append(None if s == len(SLICES) - 1 else keep.tile([P, b - a, PACK], BF16, name="quads%d" % s, tag="quads%d" % s if s < len(SLICES) - 1 else LAST_TAG, align_bytes=64))
            x_codes.append(keep.tile([P, b - a], U32, name="x_codes%d" % s, align_bytes=64)[:] if s < len(SLICES) - 2 else None)
            x_scales.append(keep.tile([P, b - a], U8, name="x_scales%d" % s, align_bytes=64))

        nc.vector.memset(warm[:], 0.0)
        nc.scalar.activation(warm[:, 1:2], warm[:, 0:1], GELU)

        tokens = xT.rearrange("(p j) t -> p j t", j=PACK)
        nc.sync.dma_start(rows[0][:], tokens[:, 0, :])
        nc.sync.dma_start(offsets[:], offs)
        nc.sync.dma_start(rows[1][:], tokens[:, 1, :])
        nc.sync.dma_start(rows[2][:], tokens[:, 2, :])
        done = 0
        for b in PIECES:
            upto = T - S + b
            nc.sync.dma_start(rows[3][:, done:upto], tokens[:, 3, done:upto])
            done = upto
        for name, src in (("w1", w1), ("w3", w3), ("w2", w2)):
            nc.sync.dma_start(raws[name][:], src.rearrange("(p j) c -> p j c", j=PACK))

        def window(s, j):
            a, b = SLICES[s]
            upto = T if j < PACK - 1 else T - S + min(e for e in PIECES if e >= b)
            return rows[j][:, 0:upto].indirect(offsets[:, a // 16 : b // 16])

        def gather_scalar(s, j):
            nc.scalar.activation(picked[s][:, j, :], window(s, j), COPY)

        def gather_vector(s, j):
            nc.vector.tensor_copy(picked[s][:, j, :], window(s, j))

        def weave(s):
            if s == len(SLICES) - 1:
                quads[s] = keep.tile([P, S - SLICES[s][0], PACK], BF16, name="quads_last", tag=LAST_TAG, align_bytes=64)
            nc.vector.tensor_copy(quads[s][:].rearrange("p (c i) j -> p c j i", i=2),
                                  picked[s][:].rearrange("p j (c i) -> p c j i", i=2))

        def place(s, j):
            nc.vector.tensor_copy(quads[s][:, :, j], picked[s][:, j, :])

        def quantise_x(s):
            if s >= len(SLICES) - 2:
                tag = "w3_rounded2" if s == len(SLICES) - 2 else "w3_rounded0"
                x_codes[s] = keep.tile([P, SLICES[s][1] - SLICES[s][0]], U32, name="x_codes%d" % s, tag=tag, align_bytes=64)[:]
            nc.vector.quantize_mx(x_codes[s].bitcast(FP8X4), x_scales[s][:], quads[s][:].rearrange("p n j -> p (n j)"))

        def dealt(name, lo, hi, t0):
            return (roundeds[name, t0][:].rearrange("p (t m j) -> p m j t", t=2, j=PACK)[:, lo:hi],
                    raws[name][:].rearrange("p j (m t) -> p m j t", t=PACK)[:, lo:hi, :, t0 : t0 + 2])

        def quantise_w(name, lo, hi):
            nc.vector.quantize_mx(w_codes[name][:, lo:hi].bitcast(FP8X4), w_scales[name][:, lo:hi],
                                  roundeds[name, lo // P][:])

        def prepare_w(name, share):
            for t0 in (2, 0):
                nc.scalar.copy(*dealt(name, 0, share, t0))
            for t0 in (2, 0) if share < P else ():
                nc.vector.tensor_copy(*dealt(name, share, P, t0))
            quantise_w(name, H // 2, H)
            quantise_w(name, 0, H // 2)

        def round_w2():
            roundeds["w2", 0] = keep.tile([P, N * PACK], BF16, name="w2_rounded", tag="w3_rounded0", align_bytes=64)
            nc.vector.tensor_copy(roundeds["w2", 0][:].rearrange("p (c i j) -> p c j i", i=2, j=PACK),
                                  raws["w2"][:].rearrange("p j (c i) -> p c j i", i=2))

        def round_w2_gpsimd(tag):
            roundeds["w2", 0] = keep.tile([P, N * PACK], BF16, name="w2_rounded_late", tag=LAST_TAG, align_bytes=64)
            nc.gpsimd.tensor_scalar(roundeds["w2", 0][:].rearrange("p (c j) -> p c j", j=PACK),
                                    raws["w2"][:].rearrange("p j c -> p c j"), 1.0, 0.0, MULT, ADD)

        def product(bank, name, i):
            s = max(k for k, (a, b) in enumerate(SLICES) if a <= i * BLOCK)
            at = i * BLOCK - SLICES[s][0]
            for t in (2, 3, 0, 1):
                cols = slice(t * P, (t + 1) * P)
                nc.tensor.matmul_mx(
                    out=bank[:, t, :],
                    lhsT=w_codes[name][:, cols].bitcast(FP8X4), lhsT_scale=w_scales[name][:, cols],
                    rhs=x_codes[s][:, at : at + BLOCK].bitcast(FP8X4), rhs_scale=x_scales[s][:, at : at + BLOCK],
                    start=True, stop=True)

        def warm_up(s):
            idle = y_banks.tile([P, N // P, 2 * BLOCK], F32, name="y_bank")
            for k in range(WARM_UPS):
                nc.tensor.matmul_mx(
                    out=idle[:, k % 2, :],
                    lhsT=x_codes[s][:, 0:P].bitcast(FP8X4), lhsT_scale=x_scales[s][:, 0:P],
                    rhs=x_codes[s][:, 0 : 2 * BLOCK].bitcast(FP8X4), rhs_scale=x_scales[s][:, 0 : 2 * BLOCK],
                    start=True, stop=True)

        def prepare_w1():
            rounded = keep.tile([P, H * PACK], BF16, name="w1_rounded", align_bytes=64)
            dst = rounded[:].rearrange("p (t m j) -> p m j t", t=PACK, j=PACK)
            src = raws["w1"][:].rearrange("p j (m t) -> p m j t", t=PACK)
            nc.scalar.copy(dst[:, 0:W1_SCALAR], src[:, 0:W1_SCALAR])
            nc.vector.tensor_copy(dst[:, W1_SCALAR:P], src[:, W1_SCALAR:P])
            return rounded

        def round_w(name, share, t0, engine):
            if engine == "s":
                nc.scalar.copy(*dealt(name, 0, share, t0))
            elif share < P:
                nc.vector.tensor_copy(*dealt(name, share, P, t0))

        gelus, linears, hiddens = {}, {}, {}

        def woven(bank):
            return bank[:].rearrange("p t (j c) -> p j c t", j=PACK)

        def gate(i):
            bank = gate_banks.tile([P, PACK, BLOCK], F32, name="gate_bank")
            product(bank, "w1", i)
            if FREE_GELUS <= i < GELU_LEAD:
                at = (i - FREE_GELUS) * BLOCK
                gelus[i] = raws["w3"][:, :, at : at + BLOCK].rearrange("p j (c t) -> p j c t", t=PACK)
            else:
                own = keep.tile([P, BLOCK * PACK], F32, name="gelu%d" % i, align_bytes=64)
                gelus[i] = own[:].rearrange("p (j c t) -> p j c t", j=PACK, t=PACK)
            nc.scalar.activation(gelus[i], woven(bank), GELU)

        def linear(i):
            linears[i] = lin_banks.tile([P, PACK, BLOCK], F32, name="lin_bank")
            product(linears[i], "w3", i)

        def multiply(i):
            q = max(k for k, (lo, hi) in enumerate(GROUPS) if lo <= i)
            lo, hi = GROUPS[q]
            if i == lo:
                hiddens[q] = keep.tile([P, (hi - lo) * BLOCK, PACK], BF16, name="hidden%d" % q, align_bytes=64)
            at = (i - lo) * BLOCK
            nc.vector.tensor_tensor(hiddens[q][:, at : at + BLOCK, :].rearrange("p (j c) t -> p j c t", j=PACK),
                                    woven(linears[i]), gelus[i], MULT)

        h_quantised = {}

        def quantise_h(q):
            lo, hi = GROUPS[q]
            n = (hi - lo) * BLOCK
            h_codes = keep.tile([P, n], U32, name="h_codes%d" % q, align_bytes=64)
            h_scales = keep.tile([P, n], U8, name="h_scales%d" % q, align_bytes=64)
            nc.vector.quantize_mx(h_codes[:].bitcast(FP8X4), h_scales[:], hiddens[q][:].rearrange("p n t -> p (n t)"))
            h_quantised[q] = (h_codes, h_scales)

        def finish(q):
            lo, hi = GROUPS[q]
            n = (hi - lo) * BLOCK
            h_codes, h_scales = h_quantised[q]
            if n == 4 * BLOCK:
                for m in range(N // P):
                    cols = slice(m * P, (m + 1) * P)
                    y = y_banks.tile([P, n], F32, name="y_bank")
                    nc.tensor.matmul_mx(
                        out=y[:],
                        lhsT=w_codes["w2"][:, cols].bitcast(FP8X4), lhsT_scale=w_scales["w2"][:, cols],
                        rhs=h_codes[:].bitcast(FP8X4), rhs_scale=h_scales[:],
                        start=True, stop=True)
                    y_out = keep.tile([P, n], F32, name="y_out%d_%d" % (q, m))
                    nc.scalar.copy(y_out[:], y[:])
                    nc.sync.dma_start(out[cols, lo * BLOCK : hi * BLOCK], y_out[:])
                return
            if q < len(GROUPS) - 3:
                y = y_banks.tile([P, N // P, n], F32, name="y_bank")
            else:
                y = gate_banks.tile([P, N // P, n], F32, name="gate_bank")
            for m in range(N // P):
                cols = slice(m * P, (m + 1) * P)
                nc.tensor.matmul_mx(
                    out=y[:, m, :],
                    lhsT=w_codes["w2"][:, cols].bitcast(FP8X4), lhsT_scale=w_scales["w2"][:, cols],
                    rhs=h_codes[:].bitcast(FP8X4), rhs_scale=h_scales[:],
                    start=True, stop=True)
            y_out = keep.tile([P, N // P, n], F32, name="y_out%d" % q)
            if q >= len(GROUPS) - VECTOR_RESULTS:
                nc.vector.tensor_copy(y_out[:], y[:])
            else:
                nc.scalar.copy(y_out[:], y[:])
            nc.sync.dma_start(out.rearrange("(m p) n -> p m n", p=P)[:, :, lo * BLOCK : hi * BLOCK], y_out[:])

        for j in range(PACK - 1):
            for s in range(EARLY_VECTOR):
                gather_scalar(s, j)
            for s in range(EARLY_VECTOR, len(SLICES)):
                gather_vector(s, j)
        gather_vector(0, 3)
        gather_scalar(1, 3)
        gather_scalar(2, 3)
        gather_scalar(3, 3)
        gather_scalar(4, 3)
        weave(0)
        weave(1)
        quantise_x(0)
        quantise_x(1)
        weave(2)
        weave(3)
        quantise_x(2)
        warm_up(2)
        round_w("w1", W1_SCALAR, 2, "s")
        round_w("w1", W1_SCALAR, 0, "s")
        round_w("w1", W1_SCALAR, 2, "v")
        round_w("w1", W1_SCALAR, 0, "v")
        quantise_w("w1", H // 2, H)
        quantise_w("w1", 0, H // 2)
        weave(4)
        round_w("w3", W3_SCALAR, 2, "s")
        round_w("w3", W3_SCALAR, 0, "s")
        round_w("w3", W3_SCALAR, 2, "v")
        round_w("w3", W3_SCALAR, 0, "v")
        quantise_w("w3", H // 2, H)
        quantise_w("w3", 0, H // 2)
        quantise_x(3)
        quantise_x(4)
        round_w2_gpsimd("quads4")
        gate(0)
        gate(1)
        linear(0)
        gate(2)
        linear(1)
        gate(3)
        linear(2)
        multiply(0)
        gate(4)
        linear(3)
        multiply(1)
        gate(5)
        linear(4)
        multiply(2)
        gate(6)
        linear(5)
        multiply(3)
        gate(7)
        linear(6)
        multiply(4)
        quantise_h(0)
        quantise_w("w2", 0, N)
        finish(0)
        gate(8)
        linear(7)
        multiply(5)
        gate(9)
        linear(8)
        multiply(6)
        quantise_h(1)
        gate(10)
        linear(9)
        multiply(7)
        finish(1)
        gate(11)
        linear(10)
        multiply(8)
        quantise_h(2)
        linear(11)
        finish(2)
        multiply(9)
        quantise_h(3)
        finish(3)
        multiply(10)
        quantise_h(4)
        finish(4)
        multiply(11)
        quantise_h(5)
        quantise_h(6)
        finish(5)
        finish(6)
